import numpy as np
import ml_dtypes


def mxq(x, axis, fmt="e4m3"):
    dtype, down = {"e4m3": (ml_dtypes.float8_e4m3fn, 7), "e5m2": (ml_dtypes.float8_e5m2, 14)}[fmt]
    v = np.moveaxis(np.asarray(x, np.float32).astype(ml_dtypes.bfloat16).astype(np.float64), axis, -1)
    blocks = v.reshape(v.shape[:-1] + (-1, 32))
    amax = np.abs(blocks).max(-1, keepdims=True)
    byte = np.maximum(np.where(amax > 0, np.frexp(amax)[1] - 1 + 127, 0) - down, 1)
    scale = np.exp2(byte - 127.0)
    codes = (blocks / scale).astype(np.float32).astype(dtype).astype(np.float64)
    return np.moveaxis((codes * scale).reshape(v.shape), -1, axis)


WIDE = False


def mx_kscale(k):
    if not WIDE:
        return np.ones(k)
    levels = np.array([10, -10, 5, -5, 0])
    if k % 512:
        return np.exp2(np.random.permutation(np.resize(levels, k // 32))).repeat(32)
    a = np.empty((k // 512, 16))
    for p in range(k // 512):
        a[p, :8] = np.random.permutation(np.resize(levels, 8))
        for g in range(8):
            far = levels[np.abs(levels - a[p, g]) >= 10]
            a[p, g + 8] = far[np.random.randint(len(far))]
    return np.exp2(a.ravel()).repeat(32)


def f64(x):
    return np.asarray(x).astype(np.float64)


def striped(idx):
    return np.tile(idx.reshape(-1, 16).T, (8, 1)).astype(np.uint16)


def unstriped(offs):
    return offs[:16].T.reshape(-1).astype(np.int64)


E2M1 = np.array([0.0, 0.5, 1.0, 1.5, 2.0, 3.0, 4.0, 6.0, -0.0, -0.5, -1.0, -1.5, -2.0, -3.0, -4.0, -6.0])


def pack_weight(w, fmt):
    k, n = w.shape
    w = f64(np.asarray(w, np.float32).astype(ml_dtypes.bfloat16)).reshape(k // 32, 32, n)
    amax = np.abs(w).max(1)
    if fmt == "e4m3":
        byte = np.frexp(amax)[1] - 1 + 127 - 7
    else:
        mant, ex = np.frexp(amax / 6.0)
        byte = np.where(mant > 0.5, ex, ex - 1) + 127
    byte = np.clip(np.where(amax > 0, byte, 1), 1, 254)
    scaled = (w * np.exp2(127.0 - byte)[:, None, :]).reshape(k, n).astype(np.float32)
    by_word = np.ascontiguousarray(scaled.reshape(k // 512, 128, 4, n).transpose(0, 1, 3, 2))
    if fmt == "e4m3":
        words = by_word.astype(ml_dtypes.float8_e4m3fn).view(np.uint8)
    else:
        c = by_word.astype(ml_dtypes.float4_e2m1fn).view(np.uint8) & 0xF
        words = (c[..., 0::2] | (c[..., 1::2] << 4)).reshape(k // 512, 128, 2 * n)
    return np.ascontiguousarray(words), np.ascontiguousarray(byte.astype(np.uint8).reshape(k // 512, 16, n))


def unpack_weight(words, scales, fmt):
    g, _, n = scales.shape
    words = np.ascontiguousarray(words).reshape(g, 128, n, -1)
    if fmt == "e4m3":
        vals = words.view(ml_dtypes.float8_e4m3fn).astype(np.float64)
    else:
        nib = np.empty((g, 128, n, 4), np.uint8)
        nib[..., 0::2] = words & 0xF
        nib[..., 1::2] = words >> 4
        vals = E2M1[nib]
    vals = vals * np.repeat(np.exp2(scales.astype(np.float64) - 127.0), 8, axis=1)[..., None]
    return vals.transpose(0, 1, 3, 2).reshape(g * 512, n)


def gelu(v):
    return 0.5 * v * (1.0 + np.tanh(np.sqrt(2.0 / np.pi) * (v + 0.044715 * v**3)))


K, T, E, C, H, N = 1536, 768, 8, 256, 512, 256
R = 4


def by_expert(wq, xq):
    return np.concatenate([wq[e].T @ xq[:, e * C:(e + 1) * C] for e in range(E)], axis=1)


def setup_inputs():
    n = np.random.standard_normal
    s = mx_kscale(K)[:, None]
    u = mx_kscale(H)
    slot_token = np.concatenate([r * (T // R) + np.random.permutation(T // R)[:C // R] for e in range(E) for r in range(R)])
    w1 = [pack_weight(m, "e2m1") for m in n((E, K, H)) / np.sqrt(K) / s[None] * u[None, None, :]]
    w2 = [pack_weight(m, "e2m1") for m in n((E, H, N)) / np.sqrt(H) / u[None, :, None]]
    x = pack_weight(n((K, T)) * s, "e4m3")
    return {
        "x_words": x[0],
        "x_scales": x[1],
        "w1_words": np.stack([m[0] for m in w1]),
        "w1_scales": np.stack([m[1] for m in w1]),
        "w2_words": np.stack([m[0] for m in w2]),
        "w2_scales": np.stack([m[1] for m in w2]),
        "offs": striped(slot_token),
    }


def reference(x_words, x_scales, w1_words, w1_scales, w2_words, w2_scales, offs):
    idx = unstriped(offs)
    w1 = np.stack([unpack_weight(w1_words[e], w1_scales[e], "e2m1") for e in range(E)])
    w2 = np.stack([unpack_weight(w2_words[e], w2_scales[e], "e2m1") for e in range(E)])
    xq = unpack_weight(x_words, x_scales, "e4m3")[:, idx]
    h = gelu(by_expert(w1, xq))
    y = by_expert(w2, mxq(h, 0, "e4m3"))
    return y.reshape(N, E, R, C // R).transpose(0, 2, 1, 3).reshape(N, E * C)

@@ -1,0 +1,237 @@
+from contextlib import ExitStack
+
+import concourse.mybir as mybir
+from concourse.masks import make_identity
+
+K, T, E, C, H, N, R = 1536, 768, 8, 256, 512, 256, 4
+FLOPS = 2 * E * C * (K * H + H * N)
+
+F32 = mybir.dt.float32
+BF16 = mybir.dt.bfloat16
+I32 = mybir.dt.int32
+U32 = mybir.dt.uint32
+U16 = mybir.dt.uint16
+U8 = mybir.dt.uint8
+FP8X4 = mybir.dt.float8_e4m3fn_x4
+FP4X4 = mybir.dt.float4_e2m1fn_x4
+GELU = mybir.ActivationFunctionType.Gelu_apprx_tanh
+
+P = 128
+PASSES = K // 512
+S = E * C
+U = C // R
+PAIR = 2 * C
+MOVED_ROWS = 112
+
+
+def tile_moe_pke_mlp_gelu_kernel(
+    tc, x_words, x_scales, w1_words, w1_scales, w2_words, w2_scales, offs, out
+):
+    nc = tc.nc
+    with ExitStack() as ctx:
+        keep = ctx.enter_context(tc.tile_pool(name="keep", bufs=1))
+        ring = ctx.enter_context(tc.tile_pool(name="ring", bufs=4))
+        gring = ctx.enter_context(tc.tile_pool(name="gring", bufs=2))
+        sring = ctx.enter_context(tc.tile_pool(name="sring", bufs=2))
+        wring = ctx.enter_context(tc.tile_pool(name="wring", bufs=8))
+        ps_a = ctx.enter_context(tc.psum_pool(name="ps_a", bufs=4))
+        ps_t = ctx.enter_context(tc.psum_pool(name="ps_t", bufs=2))
+        ps_y = ctx.enter_context(tc.psum_pool(name="ps_y", bufs=2))
+
+        lists = keep.tile([P, S // 16], U16, name="lists")
+        xs = keep.tile([P, T], U8, name="xs", align_bytes=64)
+        xw = [keep.tile([P, T], I32, name=f"xw{a}", align_bytes=64) for a in range(PASSES)]
+        w1s = keep.tile([P, E * PASSES, H], U8, name="w1s", align_bytes=64)
+        w2w = keep.tile([P, E, 2 * N], U8, name="w2w", align_bytes=64)
+        w2s = keep.tile([P, E, N], U8, name="w2s", align_bytes=64)
+        moved = [keep.tile([P, S], U8, name=f"moved{a}", align_bytes=64) for a in (1, 2)]
+        ident = keep.tile([P, P], F32, name="ident", align_bytes=64)
+        warm = keep.tile([P, 16], F32, name="warm")
+        w1w, gw, gs, hb, hq, stage, stores = {}, {}, {}, {}, {}, {}, {}
+
+        def zero(ap, engine):
+            engine.memset(ap.bitcast(I32), 0)
+
+        def load_w1_scales(e0, e1, queue):
+            src = w1_scales[e0:e1].rearrange("e s q i -> q (e s) i")
+            for r in range(4):
+                queue.dma_start(
+                    w1s[r:P:32, PASSES * e0 : PASSES * e1, :].bitcast(I32),
+                    src[r:16:4].bitcast(I32),
+                )
+
+        def load_w2_scales(queue):
+            src = w2_scales.rearrange("e s q n -> q (e s) n")
+            for r in range(4):
+                queue.dma_start(w2s[r:P:32].bitcast(I32), src[r:16:4].bitcast(I32))
+
+        def load_w1_words(e):
+            w1w[e] = wring.tile([P, PASSES, 2 * H], U8, name="w1w", align_bytes=64)
+            nc.sync.dma_start(w1w[e][:].bitcast(I32), w1_words[e].rearrange("s p b -> p s b").bitcast(I32))
+
+        def load_x_words(a):
+            nc.sync.dma_start(xw[a][:], x_words[a].rearrange("p t r -> p (t r)").bitcast(I32))
+
+        def load_w2_words(e0, e1, queue):
+            src = w2_words[e0:e1].rearrange("e s p b -> p (e s) b")
+            queue.dma_start(w2w[:, e0:e1, :].bitcast(I32), src.bitcast(I32))
+
+        def offsets(s0, s1):
+            return lists[:, s0 // 16 : s1 // 16]
+
+        def gather_expert(e, c0, c1):
+            for a in range(PASSES):
+                if c0 == 0:
+                    gw[e, a] = gring.tile([P, C], U32, name=f"gw{a}", align_bytes=64)
+                window = xw[a][:].bitcast(U32)
+                nc.vector.tensor_copy(gw[e, a][:, c0:c1], window.indirect(offsets(e * C + c0, e * C + c1)))
+
+        def gather_scales(pair, queues):
+            s0, s1 = PAIR * pair, PAIR * (pair + 1)
+            gs[pair] = sring.tile([P, PAIR], U8, name="gs", align_bytes=64)
+            nc.vector.tensor_copy(gs[pair][:], xs[:].indirect(offsets(s0, s1)))
+            for a, queue in zip((1, 2), queues):
+                queue.dma_start(
+                    moved[a - 1][0:MOVED_ROWS, s0:s1].bitcast(I32),
+                    gs[pair][4 * a : 4 * a + MOVED_ROWS, :].bitcast(I32),
+                )
+
+        def x_plane(a, s0):
+            if a == 0:
+                return gs[s0 // PAIR][:, s0 % PAIR : s0 % PAIR + P]
+            return moved[a - 1][:, s0 : s0 + P]
+
+        def layer1(e, js):
+            accs = {j: ps_a.tile([P, H], F32, name="acc") for j in js}
+            for a in range(PASSES):
+                for j in js:
+                    nc.tensor.matmul_mx(
+                        out=accs[j][:],
+                        lhsT=gw[e, a][:, j * P : (j + 1) * P].bitcast(FP8X4),
+                        lhsT_scale=x_plane(a, e * C + j * P),
+                        rhs=w1w[e][:, a, :].bitcast(FP4X4),
+                        rhs_scale=w1s[:, PASSES * e + a, :],
+                        start=(a == 0),
+                        stop=(a == PASSES - 1),
+                    )
+            for j in js:
+                h = ring.tile([P, H], BF16, name="h", align_bytes=64)
+                nc.scalar.activation(
+                    h[:].rearrange("s (u p t) -> s u p t", u=2, t=2),
+                    accs[j][:].rearrange("s (p u t) -> s u p t", u=2, t=2),
+                    GELU,
+                )
+                hb[e, j] = h
+
+        def turn(e, js, copy_out):
+            n = len(js)
+            xt = ps_t.tile([P, n, 2, P], F32, name="xt")
+            for i, j in enumerate(js):
+                pairs = hb[e, j][:].bitcast(F32)
+                for u in range(2):
+                    nc.tensor.transpose(xt[:, i, u, :], pairs[:, u * P : (u + 1) * P], ident[:])
+            ht = ring.tile([P, n * P * 4], BF16, name="ht", align_bytes=64)
+            copy_out(
+                ht[:].bitcast(F32).rearrange("p (j s u) -> p j s u", j=n, u=2),
+                xt[:].rearrange("p j u s -> p j s u"),
+            )
+            hq[e, js[0]] = ht
+
+        def finish(e, js, copy_out):
+            n = len(js) * P
+            codes = ring.tile([P, n], U32, name="codes", align_bytes=64)
+            scales = ring.tile([P, n], U8, name="scales", align_bytes=64)
+            nc.vector.quantize_mx(out=codes[:].bitcast(FP8X4), scales=scales[:], in_=hq[e, js[0]][:])
+            y = ps_y.tile([P, 2, n], F32, name="y")
+            for half in range(2):
+                nc.tensor.matmul_mx(
+                    out=y[:, half, :],
+                    lhsT=w2w[:, e, 2 * P * half : 2 * P * (half + 1)].bitcast(FP4X4),
+                    lhsT_scale=w2s[:, e, P * half : P * (half + 1)],
+                    rhs=codes[:].bitcast(FP8X4),
+                    rhs_scale=scales[:],
+                    start=True,
+                    stop=True,
+                )
+            e0, st = stage[e, js[0]]
+            copy_out(st[:, :, :, (e - e0) * U : (e - e0 + 1) * U], y[:].rearrange("p h (m u) -> p h m u", u=U))
+            if (e, js[0]) in stores:
+                e1, m0, m1 = stores[e, js[0]]
+                for half, queue in enumerate((nc.sync, nc.scalar if e == E - 1 else nc.sync)):
+                    dst = out[P * half : P * (half + 1), :].rearrange("p (m c) -> p m c", m=R)
+                    queue.dma_start(dst[:, m0:m1, e0 * U : e1 * U], st[:, half, :, :])
+
+        for e0, e1, m0, m1 in [(0, 2, 0, 4), (2, 4, 0, 4), (4, 6, 0, 4), (6, 7, 0, 4), (7, 8, 0, 2), (7, 8, 2, 4)]:
+            st_tile = keep.tile([P, 2, m1 - m0, (e1 - e0) * U], F32, name=f"stage{e0}_{m0}")
+            for e in range(e0, e1):
+                stage[e, m0 // 2] = (e0, st_tile)
+            stores[e1 - 1, m0 // 2] = (e1, m0, m1)
+
+        nc.gpsimd.memset(xs[:].bitcast(I32), 0)
+        nc.sync.dma_start(lists[:], offs)
+        load_x_words(0)
+        for q, queue in enumerate((nc.sync, nc.scalar, nc.sync, nc.scalar)):
+            queue.dma_start(xs[32 * q : 32 * q + 12].bitcast(I32), x_scales[:, 4 * q : 4 * q + 4, :].bitcast(I32))
+        w1s_flat = w1s[:].rearrange("p g i -> p (g i)")
+        zero(w1s_flat[:, : 2 * PASSES * H], nc.vector)
+        nc.vector.memset(warm[:, 0:1], 0.0)
+        nc.scalar.activation(warm[:, 8:9], warm[:, 0:1], GELU)
+        load_x_words(1)
+        load_w1_words(0)
+        load_x_words(2)
+        load_w1_scales(0, 2, nc.scalar)
+        for plane in moved:
+            zero(plane[:], nc.gpsimd)
+        gather_scales(0, (nc.scalar, nc.scalar))
+        load_w1_words(1)
+        zero(w1s_flat[:, 2 * PASSES * H :], nc.vector)
+        zero(w2s[:].rearrange("p e n -> p (e n)"), nc.vector)
+        make_identity(nc, ident[:])
+        gather_expert(0, 0, C)
+        load_w1_scales(2, 8, nc.scalar)
+        layer1(0, (0, 1))
+        gather_expert(1, 0, C)
+        gather_scales(1, (nc.sync, nc.sync))
+        load_w1_words(2)
+        load_w2_scales(nc.sync)
+        load_w2_words(0, E, nc.sync)
+        load_w1_words(3)
+        load_w1_words(4)
+        layer1(1, (0, 1))
+        turn(0, (0, 1), nc.scalar.copy)
+        gather_expert(2, 0, C)
+        gather_scales(2, (nc.sync, nc.sync))
+        load_w1_words(5)
+        layer1(2, (0, 1))
+        turn(1, (0, 1), nc.scalar.copy)
+        finish(0, (0, 1), nc.scalar.copy)
+        gather_expert(3, 0, C)
+        load_w1_words(6)
+        layer1(3, (0, 1))
+        turn(2, (0, 1), nc.scalar.copy)
+        finish(1, (0, 1), nc.scalar.copy)
+        gather_expert(4, 0, C)
+        gather_scales(3, (nc.sync, nc.sync))
+        load_w1_words(7)
+        layer1(4, (0, 1))
+        turn(3, (0, 1), nc.scalar.copy)
+        finish(2, (0, 1), nc.scalar.copy)
+        gather_expert(5, 0, C)
+        layer1(5, (0, 1))
+        turn(4, (0, 1), nc.scalar.copy)
+        finish(3, (0, 1), nc.scalar.copy)
+        gather_expert(6, 0, C)
+        layer1(6, (0, 1))
+        turn(5, (0, 1), nc.scalar.copy)
+        finish(4, (0, 1), nc.scalar.copy)
+        gather_expert(7, 0, P)
+        layer1(7, (0,))
+        turn(6, (0, 1), nc.vector.tensor_copy)
+        finish(5, (0, 1), nc.vector.tensor_copy)
+        gather_expert(7, P, C)
+        layer1(7, (1,))
+        turn(7, (0,), nc.vector.tensor_copy)
+        finish(6, (0, 1), nc.scalar.copy)
+        turn(7, (1,), nc.vector.tensor_copy)
+        finish(7, (0,), nc.scalar.copy)
+        finish(7, (1,), nc.vector.tensor_copy)

@@ -20,7 +20,8 @@ P = 128
 PASSES = K // 512
 S = E * C
 U = C // R
-PAIR = 2 * C
+CUTS = (0, 2, 5, 8)
+WINDOW = 1024
 MOVED_ROWS = 112
 
 
@@ -39,8 +40,8 @@ def tile_moe_pke_mlp_gelu_kernel(
         ps_y = ctx.enter_context(tc.psum_pool(name="ps_y", bufs=2))
 
         lists = keep.tile([P, S // 16], U16, name="lists")
-        xs = keep.tile([P, T], U8, name="xs", align_bytes=64)
-        xw = [keep.tile([P, T], I32, name=f"xw{a}", align_bytes=64) for a in range(PASSES)]
+        xs = keep.tile([P, WINDOW], U8, name="xs", align_bytes=64)
+        xw = keep.tile([P, PASSES, T], I32, name="xw", align_bytes=64)
         w1s = keep.tile([P, E * PASSES, H], U8, name="w1s", align_bytes=64)
         w2w = keep.tile([P, E, 2 * N], U8, name="w2w", align_bytes=64)
         w2s = keep.tile([P, E, N], U8, name="w2s", align_bytes=64)
@@ -52,25 +53,27 @@ def tile_moe_pke_mlp_gelu_kernel(
         def zero(ap, engine):
             engine.memset(ap.bitcast(I32), 0)
 
-        def load_w1_scales(e0, e1, queue):
+        def load_w1_scales(e0, e1, queues):
             src = w1_scales[e0:e1].rearrange("e s q i -> q (e s) i")
-            for r in range(4):
+            for q, queue in zip((0, 2, 1, 3), queues):
                 queue.dma_start(
-                    w1s[r:P:32, PASSES * e0 : PASSES * e1, :].bitcast(I32),
-                    src[r:16:4].bitcast(I32),
+                    w1s[32 * q : 32 * q + 4, PASSES * e0 : PASSES * e1, :].bitcast(I32),
+                    src[4 * q : 4 * q + 4].bitcast(I32),
                 )
 
-        def load_w2_scales(queue):
+        def load_w2_scales(queues):
             src = w2_scales.rearrange("e s q n -> q (e s) n")
-            for r in range(4):
-                queue.dma_start(w2s[r:P:32].bitcast(I32), src[r:16:4].bitcast(I32))
+            for q, queue in zip((0, 2, 1, 3), queues):
+                queue.dma_start(w2s[32 * q : 32 * q + 4].bitcast(I32), src[4 * q : 4 * q + 4].bitcast(I32))
 
-        def load_w1_words(e):
-            w1w[e] = wring.tile([P, PASSES, 2 * H], U8, name="w1w", align_bytes=64)
-            nc.sync.dma_start(w1w[e][:].bitcast(I32), w1_words[e].rearrange("s p b -> p s b").bitcast(I32))
+        def load_w1_words(e0, e1):
+            words = keep.tile([P, (e1 - e0) * PASSES, 2 * H], U8, name=f"w1w{e0}", align_bytes=64)
+            nc.sync.dma_start(words[:].bitcast(I32), w1_words[e0:e1].rearrange("e s p b -> p (e s) b").bitcast(I32))
+            for e in range(e0, e1):
+                w1w[e] = words[:, (e - e0) * PASSES : (e - e0 + 1) * PASSES, :]
 
-        def load_x_words(a):
-            nc.sync.dma_start(xw[a][:], x_words[a].rearrange("p t r -> p (t r)").bitcast(I32))
+        def load_x_words(a0, a1):
+            nc.sync.dma_start(xw[:, a0:a1, :], x_words[a0:a1].rearrange("a p t r -> p a (t r)").bitcast(I32))
 
         def load_w2_words(e0, e1, queue):
             src = w2_words[e0:e1].rearrange("e s p b -> p (e s) b")
@@ -83,12 +86,12 @@ def tile_moe_pke_mlp_gelu_kernel(
             for a in range(PASSES):
                 if c0 == 0:
                     gw[e, a] = gring.tile([P, C], U32, name=f"gw{a}", align_bytes=64)
-                window = xw[a][:].bitcast(U32)
+                window = xw[:, a, :].bitcast(U32)
                 nc.vector.tensor_copy(gw[e, a][:, c0:c1], window.indirect(offsets(e * C + c0, e * C + c1)))
 
         def gather_scales(pair, queues):
-            s0, s1 = PAIR * pair, PAIR * (pair + 1)
-            gs[pair] = sring.tile([P, PAIR], U8, name="gs", align_bytes=64)
+            s0, s1 = C * CUTS[pair], C * CUTS[pair + 1]
+            gs[pair] = sring.tile([P, s1 - s0], U8, name="gs", align_bytes=64)
             nc.vector.tensor_copy(gs[pair][:], xs[:].indirect(offsets(s0, s1)))
             for a, queue in zip((1, 2), queues):
                 queue.dma_start(
@@ -98,7 +101,9 @@ def tile_moe_pke_mlp_gelu_kernel(
 
         def x_plane(a, s0):
             if a == 0:
-                return gs[s0 // PAIR][:, s0 % PAIR : s0 % PAIR + P]
+                pair = max(i for i in range(len(CUTS) - 1) if C * CUTS[i] <= s0)
+                c0 = s0 - C * CUTS[pair]
+                return gs[pair][:, c0 : c0 + P]
             return moved[a - 1][:, s0 : s0 + P]
 
         def layer1(e, js):
@@ -142,7 +147,7 @@ def tile_moe_pke_mlp_gelu_kernel(
             codes = ring.tile([P, n], U32, name="codes", align_bytes=64)
             scales = ring.tile([P, n], U8, name="scales", align_bytes=64)
             nc.vector.quantize_mx(out=codes[:].bitcast(FP8X4), scales=scales[:], in_=hq[e, js[0]][:])
-            y = ps_y.tile([P, 2, n], F32, name="y")
+            y = ps_a.tile([P, 2, n], F32, name="acc") if e == E - 1 else ps_y.tile([P, 2, n], F32, name="y")
             for half in range(2):
                 nc.tensor.matmul_mx(
                     out=y[:, half, :],
@@ -167,71 +172,67 @@ def tile_moe_pke_mlp_gelu_kernel(
                 stage[e, m0 // 2] = (e0, st_tile)
             stores[e1 - 1, m0 // 2] = (e1, m0, m1)
 
+        w1s_flat = w1s[:].rearrange("p g i -> p (g i)")
         nc.gpsimd.memset(xs[:].bitcast(I32), 0)
         nc.sync.dma_start(lists[:], offs)
-        load_x_words(0)
+        load_x_words(0, 1)
         for q, queue in enumerate((nc.sync, nc.scalar, nc.sync, nc.scalar)):
-            queue.dma_start(xs[32 * q : 32 * q + 12].bitcast(I32), x_scales[:, 4 * q : 4 * q + 4, :].bitcast(I32))
-        w1s_flat = w1s[:].rearrange("p g i -> p (g i)")
-        zero(w1s_flat[:, : 2 * PASSES * H], nc.vector)
+            queue.dma_start(xs[32 * q : 32 * q + 12, :T].bitcast(I32), x_scales[:, 4 * q : 4 * q + 4, :].bitcast(I32))
+        zero(w1s_flat[:, : 3 * PASSES * H], nc.vector)
+        make_identity(nc, ident[:])
+        load_w1_scales(0, 3, (nc.scalar, nc.sync, nc.scalar, nc.sync))
+        load_w1_words(0, 1)
+        load_x_words(1, 3)
         nc.vector.memset(warm[:, 0:1], 0.0)
         nc.scalar.activation(warm[:, 8:9], warm[:, 0:1], GELU)
-        load_x_words(1)
-        load_w1_words(0)
-        load_x_words(2)
-        load_w1_scales(0, 2, nc.scalar)
         for plane in moved:
-            zero(plane[:], nc.gpsimd)
-        gather_scales(0, (nc.scalar, nc.scalar))
-        load_w1_words(1)
-        zero(w1s_flat[:, 2 * PASSES * H :], nc.vector)
-        zero(w2s[:].rearrange("p e n -> p (e n)"), nc.vector)
-        make_identity(nc, ident[:])
+            zero(plane[:], nc.vector)
+        gather_scales(0, (nc.scalar, nc.sync))
+        load_w1_words(1, 2)
+        zero(w1s_flat[:, 3 * PASSES * H :], nc.vector)
+        zero(w2s[:].rearrange("p e n -> p (e n)"), nc.gpsimd)
         gather_expert(0, 0, C)
-        load_w1_scales(2, 8, nc.scalar)
+        load_w1_scales(3, 5, (nc.sync, nc.sync, nc.sync, nc.sync))
         layer1(0, (0, 1))
         gather_expert(1, 0, C)
-        gather_scales(1, (nc.sync, nc.sync))
-        load_w1_words(2)
-        load_w2_scales(nc.sync)
+        load_w1_words(2, 4)
+        load_w2_scales((nc.sync, nc.sync, nc.sync, nc.sync))
         load_w2_words(0, E, nc.sync)
-        load_w1_words(3)
-        load_w1_words(4)
+        load_w1_words(4, 6)
+        load_w1_words(6, 8)
+        load_w1_scales(5, E, (nc.sync, nc.sync, nc.sync, nc.sync))
         layer1(1, (0, 1))
         turn(0, (0, 1), nc.scalar.copy)
+        gather_scales(1, (nc.scalar, nc.scalar))
         gather_expert(2, 0, C)
-        gather_scales(2, (nc.sync, nc.sync))
-        load_w1_words(5)
         layer1(2, (0, 1))
         turn(1, (0, 1), nc.scalar.copy)
-        finish(0, (0, 1), nc.scalar.copy)
+        gather_scales(2, (nc.sync, nc.sync))
         gather_expert(3, 0, C)
-        load_w1_words(6)
         layer1(3, (0, 1))
         turn(2, (0, 1), nc.scalar.copy)
-        finish(1, (0, 1), nc.scalar.copy)
+        finish(0, (0, 1), nc.scalar.copy)
         gather_expert(4, 0, C)
-        gather_scales(3, (nc.sync, nc.sync))
-        load_w1_words(7)
         layer1(4, (0, 1))
         turn(3, (0, 1), nc.scalar.copy)
-        finish(2, (0, 1), nc.scalar.copy)
+        finish(1, (0, 1), nc.scalar.copy)
         gather_expert(5, 0, C)
         layer1(5, (0, 1))
         turn(4, (0, 1), nc.scalar.copy)
-        finish(3, (0, 1), nc.scalar.copy)
+        finish(2, (0, 1), nc.scalar.copy)
         gather_expert(6, 0, C)
         layer1(6, (0, 1))
-        turn(5, (0, 1), nc.scalar.copy)
-        finish(4, (0, 1), nc.scalar.copy)
+        turn(5, (0, 1), nc.vector.tensor_copy)
+        finish(3, (0, 1), nc.vector.tensor_copy)
+        finish(4, (0, 1), nc.vector.tensor_copy)
         gather_expert(7, 0, P)
         layer1(7, (0,))
         turn(6, (0, 1), nc.vector.tensor_copy)
-        finish(5, (0, 1), nc.vector.tensor_copy)
+        finish(5, (0, 1), nc.scalar.copy)
         gather_expert(7, P, C)
         layer1(7, (1,))
         turn(7, (0,), nc.vector.tensor_copy)
         finish(6, (0, 1), nc.scalar.copy)
-        turn(7, (1,), nc.vector.tensor_copy)
-        finish(7, (0,), nc.scalar.copy)
-        finish(7, (1,), nc.vector.tensor_copy)
+        finish(7, (0,), nc.vector.tensor_copy)
+        turn(7, (1,), nc.scalar.copy)
+        finish(7, (1,), nc.scalar.copy)

@@ -41,7 +41,7 @@ def tile_moe_pke_mlp_gelu_kernel(
 
         lists = keep.tile([P, S // 16], U16, name="lists")
         xs = keep.tile([P, WINDOW], U8, name="xs", align_bytes=64)
-        xw = keep.tile([P, PASSES, T], I32, name="xw", align_bytes=64)
+        xw = [keep.tile([P, T], I32, name=f"xw{a}", align_bytes=64) for a in range(PASSES)]
         w1s = keep.tile([P, E * PASSES, H], U8, name="w1s", align_bytes=64)
         w2w = keep.tile([P, E, 2 * N], U8, name="w2w", align_bytes=64)
         w2s = keep.tile([P, E, N], U8, name="w2s", align_bytes=64)
@@ -72,8 +72,8 @@ def tile_moe_pke_mlp_gelu_kernel(
             for e in range(e0, e1):
                 w1w[e] = words[:, (e - e0) * PASSES : (e - e0 + 1) * PASSES, :]
 
-        def load_x_words(a0, a1):
-            nc.sync.dma_start(xw[:, a0:a1, :], x_words[a0:a1].rearrange("a p t r -> p a (t r)").bitcast(I32))
+        def load_x_words(a):
+            nc.sync.dma_start(xw[a][:], x_words[a].rearrange("p t r -> p (t r)").bitcast(I32))
 
         def load_w2_words(e0, e1, queue):
             src = w2_words[e0:e1].rearrange("e s p b -> p (e s) b")
@@ -86,7 +86,7 @@ def tile_moe_pke_mlp_gelu_kernel(
             for a in range(PASSES):
                 if c0 == 0:
                     gw[e, a] = gring.tile([P, C], U32, name=f"gw{a}", align_bytes=64)
-                window = xw[:, a, :].bitcast(U32)
+                window = xw[a][:].bitcast(U32)
                 nc.vector.tensor_copy(gw[e, a][:, c0:c1], window.indirect(offsets(e * C + c0, e * C + c1)))
 
         def gather_scales(pair, queues):
@@ -166,6 +166,27 @@ def tile_moe_pke_mlp_gelu_kernel(
                     dst = out[P * half : P * (half + 1), :].rearrange("p (m c) -> p m c", m=R)
                     queue.dma_start(dst[:, m0:m1, e0 * U : e1 * U], st[:, half, :, :])
 
+        def finish_last():
+            e = E - 1
+            codes = ring.tile([P, P], U32, name="codes", align_bytes=64)
+            scales = ring.tile([P, P], U8, name="scales", align_bytes=64)
+            nc.vector.quantize_mx(out=codes[:].bitcast(FP8X4), scales=scales[:], in_=hq[e, 1][:])
+            st = stage[e, 1][1]
+            for half, copy_out, queue in ((0, nc.vector.tensor_copy, nc.sync), (1, nc.scalar.copy, nc.scalar)):
+                y = ps_a.tile([P, P], F32, name="acc")
+                nc.tensor.matmul_mx(
+                    out=y[:],
+                    lhsT=w2w[:, e, 2 * P * half : 2 * P * (half + 1)].bitcast(FP4X4),
+                    lhsT_scale=w2s[:, e, P * half : P * (half + 1)],
+                    rhs=codes[:].bitcast(FP8X4),
+                    rhs_scale=scales[:],
+                    start=True,
+                    stop=True,
+                )
+                copy_out(st[:, half, :, :], y[:].rearrange("p (m u) -> p m u", u=U))
+                dst = out[P * half : P * (half + 1), :].rearrange("p (m c) -> p m c", m=R)
+                queue.dma_start(dst[:, 2:4, e * U : E * U], st[:, half, :, :])
+
         for e0, e1, m0, m1 in [(0, 2, 0, 4), (2, 4, 0, 4), (4, 6, 0, 4), (6, 7, 0, 4), (7, 8, 0, 2), (7, 8, 2, 4)]:
             st_tile = keep.tile([P, 2, m1 - m0, (e1 - e0) * U], F32, name=f"stage{e0}_{m0}")
             for e in range(e0, e1):
@@ -175,40 +196,42 @@ def tile_moe_pke_mlp_gelu_kernel(
         w1s_flat = w1s[:].rearrange("p g i -> p (g i)")
         nc.gpsimd.memset(xs[:].bitcast(I32), 0)
         nc.sync.dma_start(lists[:], offs)
-        load_x_words(0, 1)
-        for q, queue in enumerate((nc.sync, nc.scalar, nc.sync, nc.scalar)):
+        load_x_words(0)
+        for q, queue in enumerate((nc.scalar, nc.sync, nc.scalar, nc.sync)):
             queue.dma_start(xs[32 * q : 32 * q + 12, :T].bitcast(I32), x_scales[:, 4 * q : 4 * q + 4, :].bitcast(I32))
         zero(w1s_flat[:, : 3 * PASSES * H], nc.vector)
         make_identity(nc, ident[:])
-        load_w1_scales(0, 3, (nc.scalar, nc.sync, nc.scalar, nc.sync))
+        load_w1_scales(0, 3, (nc.scalar, nc.scalar, nc.scalar, nc.scalar))
         load_w1_words(0, 1)
-        load_x_words(1, 3)
+        load_x_words(1)
+        load_x_words(2)
         nc.vector.memset(warm[:, 0:1], 0.0)
         nc.scalar.activation(warm[:, 8:9], warm[:, 0:1], GELU)
         for plane in moved:
             zero(plane[:], nc.vector)
-        gather_scales(0, (nc.scalar, nc.sync))
+        gather_scales(0, (nc.scalar, nc.scalar))
         load_w1_words(1, 2)
         zero(w1s_flat[:, 3 * PASSES * H :], nc.vector)
-        zero(w2s[:].rearrange("p e n -> p (e n)"), nc.gpsimd)
+        zero(w2s[:].rearrange("p e n -> p (e n)"), nc.vector)
         gather_expert(0, 0, C)
-        load_w1_scales(3, 5, (nc.sync, nc.sync, nc.sync, nc.sync))
+        gather_scales(1, (nc.scalar, nc.scalar))
+        load_w1_scales(3, 5, (nc.scalar, nc.sync, nc.scalar, nc.sync))
+        load_w1_words(2, 3)
+        load_w2_scales((nc.scalar, nc.sync, nc.scalar, nc.sync))
+        load_w1_words(3, 5)
+        load_w2_words(0, 4, nc.sync)
         layer1(0, (0, 1))
         gather_expert(1, 0, C)
-        load_w1_words(2, 4)
-        load_w2_scales((nc.sync, nc.sync, nc.sync, nc.sync))
-        load_w2_words(0, E, nc.sync)
-        load_w1_words(4, 6)
-        load_w1_words(6, 8)
         load_w1_scales(5, E, (nc.sync, nc.sync, nc.sync, nc.sync))
+        load_w1_words(5, 8)
+        load_w2_words(4, E, nc.sync)
         layer1(1, (0, 1))
         turn(0, (0, 1), nc.scalar.copy)
-        gather_scales(1, (nc.scalar, nc.scalar))
         gather_expert(2, 0, C)
         layer1(2, (0, 1))
         turn(1, (0, 1), nc.scalar.copy)
-        gather_scales(2, (nc.sync, nc.sync))
         gather_expert(3, 0, C)
+        gather_scales(2, (nc.sync, nc.sync))
         layer1(3, (0, 1))
         turn(2, (0, 1), nc.scalar.copy)
         finish(0, (0, 1), nc.scalar.copy)
@@ -220,19 +243,19 @@ def tile_moe_pke_mlp_gelu_kernel(
         layer1(5, (0, 1))
         turn(4, (0, 1), nc.scalar.copy)
         finish(2, (0, 1), nc.scalar.copy)
+        finish(3, (0, 1), nc.scalar.copy)
         gather_expert(6, 0, C)
         layer1(6, (0, 1))
         turn(5, (0, 1), nc.vector.tensor_copy)
-        finish(3, (0, 1), nc.vector.tensor_copy)
-        finish(4, (0, 1), nc.vector.tensor_copy)
+        finish(4, (0, 1), nc.scalar.copy)
         gather_expert(7, 0, P)
         layer1(7, (0,))
         turn(6, (0, 1), nc.vector.tensor_copy)
-        finish(5, (0, 1), nc.scalar.copy)
+        finish(5, (0, 1), nc.vector.tensor_copy)
         gather_expert(7, P, C)
         layer1(7, (1,))
-        turn(7, (0,), nc.vector.tensor_copy)
-        finish(6, (0, 1), nc.scalar.copy)
-        finish(7, (0,), nc.vector.tensor_copy)
+        turn(7, (0,), nc.scalar.copy)
+        finish(6, (0, 1), nc.vector.tensor_copy)
+        finish(7, (0,), nc.scalar.copy)
         turn(7, (1,), nc.scalar.copy)
-        finish(7, (1,), nc.scalar.copy)
+        finish_last()

@@ -20,9 +20,11 @@ P = 128
 PASSES = K // 512
 S = E * C
 U = C // R
-CUTS = (0, 2, 5, 8)
+CUTS = (0, 3, 6, 8)
 WINDOW = 1024
-MOVED_ROWS = 112
+W1_WORD_GROUPS = ((0, 1), (1, 2), (2, 3), (3, 4), (4, 5), (5, 6), (6, 8))
+W1_SCALE_GROUPS = ((0, 2), (2, 4), (4, 6), (6, 8))
+STORE_GROUPS = ((0, 2), (2, 4), (4, 6), (6, 7))
 
 
 def tile_moe_pke_mlp_gelu_kernel(
@@ -31,231 +33,219 @@ def tile_moe_pke_mlp_gelu_kernel(
     nc = tc.nc
     with ExitStack() as ctx:
         keep = ctx.enter_context(tc.tile_pool(name="keep", bufs=1))
-        ring = ctx.enter_context(tc.tile_pool(name="ring", bufs=4))
-        gring = ctx.enter_context(tc.tile_pool(name="gring", bufs=2))
-        sring = ctx.enter_context(tc.tile_pool(name="sring", bufs=2))
-        wring = ctx.enter_context(tc.tile_pool(name="wring", bufs=8))
-        ps_a = ctx.enter_context(tc.psum_pool(name="ps_a", bufs=4))
-        ps_t = ctx.enter_context(tc.psum_pool(name="ps_t", bufs=2))
-        ps_y = ctx.enter_context(tc.psum_pool(name="ps_y", bufs=2))
+        psum = ctx.enter_context(tc.psum_pool(name="psum", bufs=1))
 
+        def sbuf(shape, dtype, name):
+            return keep.tile(shape, dtype, name=name, align_bytes=64)
+
+        banks = [psum.tile([P, 512], F32, name=f"bank{b}") for b in range(8)]
         lists = keep.tile([P, S // 16], U16, name="lists")
-        xs = keep.tile([P, WINDOW], U8, name="xs", align_bytes=64)
-        xw = [keep.tile([P, T], I32, name=f"xw{a}", align_bytes=64) for a in range(PASSES)]
-        w1s = keep.tile([P, E * PASSES, H], U8, name="w1s", align_bytes=64)
-        w2w = keep.tile([P, E, 2 * N], U8, name="w2w", align_bytes=64)
-        w2s = keep.tile([P, E, N], U8, name="w2s", align_bytes=64)
-        moved = [keep.tile([P, S], U8, name=f"moved{a}", align_bytes=64) for a in (1, 2)]
-        ident = keep.tile([P, P], F32, name="ident", align_bytes=64)
-        warm = keep.tile([P, 16], F32, name="warm")
-        w1w, gw, gs, hb, hq, stage, stores = {}, {}, {}, {}, {}, {}, {}
+        xs = sbuf([P, WINDOW], U8, "xs")
+        xw01 = sbuf([P, 2, T], I32, "xw01")
+        xw2 = sbuf([P, T], I32, "xw2")
+        windows = [xw01[:, 0, :], xw01[:, 1, :], xw2[:]]
+        w1w = [sbuf([P, (e1 - e0) * PASSES, 2 * H], U8, f"w1w{e0}") for e0, e1 in W1_WORD_GROUPS]
+        w1s = [sbuf([P, (e1 - e0) * PASSES, H], U8, f"w1s{e0}") for e0, e1 in W1_SCALE_GROUPS]
+        w2w = sbuf([P, E, 2 * N], U8, "w2w")
+        w2s = sbuf([P, E, N], U8, "w2s")
+        gw = [[sbuf([P, C], U32, f"gw{s}_{a}") for a in range(PASSES)] for s in range(2)]
+        gs = sbuf([P, 6 * C - P], U8, "gs")
+        gs_start = (3 * C - P, C, 0)
+        moved = [sbuf([P, S], U8, f"moved{a}") for a in (1, 2)]
+        ident = sbuf([P, P], F32, "ident")
+        hb = {(e, j): sbuf([P, H], BF16, f"h{e}_{j}") for e in range(E) for j in range(2)}
+        ht = [sbuf([P, 4 * C], BF16, f"ht{e}") for e in range(E)]
+        codes = [sbuf([P, C], U32, f"codes{e}") for e in range(E)]
+        scales = [sbuf([P, C], U8, f"scales{e}") for e in range(E)]
+        stage = [keep.tile([P, 2, R, (e1 - e0) * U], F32, name=f"stage{e0}") for e0, e1 in STORE_GROUPS]
+        last = [[keep.tile([P, 2, U], F32, name=f"last{j}_{half}") for half in range(2)] for j in range(2)]
+
+        def group_of(groups, e):
+            return [g for g, (e0, e1) in enumerate(groups) if e0 <= e < e1][0]
 
         def zero(ap, engine):
             engine.memset(ap.bitcast(I32), 0)
 
-        def load_w1_scales(e0, e1, queues):
-            src = w1_scales[e0:e1].rearrange("e s q i -> q (e s) i")
-            for q, queue in zip((0, 2, 1, 3), queues):
-                queue.dma_start(
-                    w1s[32 * q : 32 * q + 4, PASSES * e0 : PASSES * e1, :].bitcast(I32),
-                    src[4 * q : 4 * q + 4].bitcast(I32),
-                )
+        def load_xs_pass0(quad, queue):
+            queue.dma_start(xs[32 * quad : 32 * quad + 4, :T].bitcast(I32), x_scales[0, 4 * quad : 4 * quad + 4, :].bitcast(I32))
 
-        def load_w2_scales(queues):
+        def load_xs_rest(q, queue):
+            src = x_scales.rearrange("a (h q r) t -> (a h) q r t", h=2, q=2)
+            queue.dma_start(xs[32 * q + 4 : 32 * q + 20, :T].bitcast(I32), src[2:6, q].bitcast(I32))
+
+        def load_w1_scales(g):
+            e0, e1 = W1_SCALE_GROUPS[g]
+            src = w1_scales[e0:e1].rearrange("e s q i -> q (e s) i")
+            for q in (0, 2, 1, 3):
+                nc.sync.dma_start(w1s[g][32 * q : 32 * q + 4].bitcast(I32), src[4 * q : 4 * q + 4].bitcast(I32))
+
+        def load_w2_scales(queue):
             src = w2_scales.rearrange("e s q n -> q (e s) n")
-            for q, queue in zip((0, 2, 1, 3), queues):
+            for q in (0, 2, 1, 3):
                 queue.dma_start(w2s[32 * q : 32 * q + 4].bitcast(I32), src[4 * q : 4 * q + 4].bitcast(I32))
 
-        def load_w1_words(e0, e1):
-            words = keep.tile([P, (e1 - e0) * PASSES, 2 * H], U8, name=f"w1w{e0}", align_bytes=64)
-            nc.sync.dma_start(words[:].bitcast(I32), w1_words[e0:e1].rearrange("e s p b -> p (e s) b").bitcast(I32))
-            for e in range(e0, e1):
-                w1w[e] = words[:, (e - e0) * PASSES : (e - e0 + 1) * PASSES, :]
-
-        def load_x_words(a):
-            nc.sync.dma_start(xw[a][:], x_words[a].rearrange("p t r -> p (t r)").bitcast(I32))
-
-        def load_w2_words(e0, e1, queue):
-            src = w2_words[e0:e1].rearrange("e s p b -> p (e s) b")
-            queue.dma_start(w2w[:, e0:e1, :].bitcast(I32), src.bitcast(I32))
+        def load_w1_words(g):
+            e0, e1 = W1_WORD_GROUPS[g]
+            nc.sync.dma_start(w1w[g][:].bitcast(I32), w1_words[e0:e1].rearrange("e s p b -> p (e s) b").bitcast(I32))
 
         def offsets(s0, s1):
             return lists[:, s0 // 16 : s1 // 16]
 
-        def gather_expert(e, c0, c1):
-            for a in range(PASSES):
-                if c0 == 0:
-                    gw[e, a] = gring.tile([P, C], U32, name=f"gw{a}", align_bytes=64)
-                window = xw[a][:].bitcast(U32)
-                nc.vector.tensor_copy(gw[e, a][:, c0:c1], window.indirect(offsets(e * C + c0, e * C + c1)))
+        def pass_order(e):
+            return (0, 1, 2) if e < 2 else (2, 1, 0)
 
-        def gather_scales(pair, queues):
-            s0, s1 = C * CUTS[pair], C * CUTS[pair + 1]
-            gs[pair] = sring.tile([P, s1 - s0], U8, name="gs", align_bytes=64)
-            nc.vector.tensor_copy(gs[pair][:], xs[:].indirect(offsets(s0, s1)))
-            for a, queue in zip((1, 2), queues):
-                queue.dma_start(
-                    moved[a - 1][0:MOVED_ROWS, s0:s1].bitcast(I32),
-                    gs[pair][4 * a : 4 * a + MOVED_ROWS, :].bitcast(I32),
-                )
+        def gather_words(e):
+            for a in pass_order(e):
+                nc.vector.tensor_copy(gw[e % 2][a][:], windows[a].bitcast(U32).indirect(offsets(e * C, (e + 1) * C)))
+
+        def gather_scales(c):
+            s0, s1 = C * CUTS[c], C * CUTS[c + 1]
+            cols = slice(gs_start[c], gs_start[c] + s1 - s0)
+            nc.vector.tensor_copy(gs[:, cols], xs[:].indirect(offsets(s0, s1)))
+            for a in (1, 2):
+                for h in range(2):
+                    row = 4 + 8 * (a - 1) + 4 * h
+                    nc.sync.dma_start(
+                        moved[a - 1][64 * h : 64 * h + 64, s0:s1].bitcast(I32),
+                        gs[row : row + 64, cols].bitcast(I32),
+                    )
 
         def x_plane(a, s0):
             if a == 0:
-                pair = max(i for i in range(len(CUTS) - 1) if C * CUTS[i] <= s0)
-                c0 = s0 - C * CUTS[pair]
-                return gs[pair][:, c0 : c0 + P]
+                c = max(i for i in range(len(CUTS) - 1) if C * CUTS[i] <= s0)
+                c0 = gs_start[c] + s0 - C * CUTS[c]
+                return gs[:, c0 : c0 + P]
             return moved[a - 1][:, s0 : s0 + P]
 
-        def layer1(e, js):
-            accs = {j: ps_a.tile([P, H], F32, name="acc") for j in js}
-            for a in range(PASSES):
-                for j in js:
-                    nc.tensor.matmul_mx(
-                        out=accs[j][:],
-                        lhsT=gw[e, a][:, j * P : (j + 1) * P].bitcast(FP8X4),
-                        lhsT_scale=x_plane(a, e * C + j * P),
-                        rhs=w1w[e][:, a, :].bitcast(FP4X4),
-                        rhs_scale=w1s[:, PASSES * e + a, :],
-                        start=(a == 0),
-                        stop=(a == PASSES - 1),
-                    )
-            for j in js:
-                h = ring.tile([P, H], BF16, name="h", align_bytes=64)
-                nc.scalar.activation(
-                    h[:].rearrange("s (u p t) -> s u p t", u=2, t=2),
-                    accs[j][:].rearrange("s (p u t) -> s u p t", u=2, t=2),
-                    GELU,
-                )
-                hb[e, j] = h
+        def acc_bank(e, j):
+            return banks[2 * (e % 2) + j]
 
-        def turn(e, js, copy_out):
-            n = len(js)
-            xt = ps_t.tile([P, n, 2, P], F32, name="xt")
+        def layer1(e, j):
+            gwords, gscales = group_of(W1_WORD_GROUPS, e), group_of(W1_SCALE_GROUPS, e)
+            acc = acc_bank(e, j)
+            for a in pass_order(e):
+                nc.tensor.matmul_mx(
+                    out=acc[:],
+                    lhsT=gw[e % 2][a][:, j * P : (j + 1) * P].bitcast(FP8X4),
+                    lhsT_scale=x_plane(a, e * C + j * P),
+                    rhs=w1w[gwords][:, (e - W1_WORD_GROUPS[gwords][0]) * PASSES + a, :].bitcast(FP4X4),
+                    rhs_scale=w1s[gscales][:, (e - W1_SCALE_GROUPS[gscales][0]) * PASSES + a, :],
+                    start=(a == pass_order(e)[0]),
+                    stop=(a == pass_order(e)[-1]),
+                )
+            nc.scalar.activation(
+                hb[e, j][:].rearrange("s (u p t) -> s u p t", u=2, t=2),
+                acc[:].rearrange("s (p u t) -> s u p t", u=2, t=2),
+                GELU,
+            )
+
+        def turn(e, bank, copy_out, js=(0, 1)):
+            cols = slice(js[0] * P, (js[-1] + 1) * P)
+            xt = bank[:, : 2 * P * len(js)].rearrange("p (j u s) -> p j u s", u=2, s=P)
             for i, j in enumerate(js):
                 pairs = hb[e, j][:].bitcast(F32)
                 for u in range(2):
                     nc.tensor.transpose(xt[:, i, u, :], pairs[:, u * P : (u + 1) * P], ident[:])
-            ht = ring.tile([P, n * P * 4], BF16, name="ht", align_bytes=64)
+            words = ht[e][:, 4 * cols.start : 4 * cols.stop]
             copy_out(
-                ht[:].bitcast(F32).rearrange("p (j s u) -> p j s u", j=n, u=2),
-                xt[:].rearrange("p j u s -> p j s u"),
+                words.bitcast(F32).rearrange("p (j s u) -> p j s u", s=P, u=2),
+                xt.rearrange("p j u s -> p j s u"),
             )
-            hq[e, js[0]] = ht
+            nc.vector.quantize_mx(out=codes[e][:, cols].bitcast(FP8X4), scales=scales[e][:, cols], in_=words)
 
-        def finish(e, js, copy_out):
-            n = len(js) * P
-            codes = ring.tile([P, n], U32, name="codes", align_bytes=64)
-            scales = ring.tile([P, n], U8, name="scales", align_bytes=64)
-            nc.vector.quantize_mx(out=codes[:].bitcast(FP8X4), scales=scales[:], in_=hq[e, js[0]][:])
-            y = ps_a.tile([P, 2, n], F32, name="acc") if e == E - 1 else ps_y.tile([P, 2, n], F32, name="y")
+        def layer2_half(e, half, y, cols):
+            nc.tensor.matmul_mx(
+                out=y,
+                lhsT=w2w[:, e, 2 * P * half : 2 * P * (half + 1)].bitcast(FP4X4),
+                lhsT_scale=w2s[:, e, P * half : P * (half + 1)],
+                rhs=codes[e][:, cols].bitcast(FP8X4),
+                rhs_scale=scales[e][:, cols],
+                start=True,
+                stop=True,
+            )
+
+        def out_rows(half):
+            return out[P * half : P * (half + 1), :].rearrange("p (m c) -> p m c", m=R)
+
+        def layer2(e, bank, copy_out):
+            g = group_of(STORE_GROUPS, e)
+            e0, e1 = STORE_GROUPS[g]
             for half in range(2):
-                nc.tensor.matmul_mx(
-                    out=y[:, half, :],
-                    lhsT=w2w[:, e, 2 * P * half : 2 * P * (half + 1)].bitcast(FP4X4),
-                    lhsT_scale=w2s[:, e, P * half : P * (half + 1)],
-                    rhs=codes[:].bitcast(FP8X4),
-                    rhs_scale=scales[:],
-                    start=True,
-                    stop=True,
-                )
-            e0, st = stage[e, js[0]]
-            copy_out(st[:, :, :, (e - e0) * U : (e - e0 + 1) * U], y[:].rearrange("p h (m u) -> p h m u", u=U))
-            if (e, js[0]) in stores:
-                e1, m0, m1 = stores[e, js[0]]
-                for half, queue in enumerate((nc.sync, nc.scalar if e == E - 1 else nc.sync)):
-                    dst = out[P * half : P * (half + 1), :].rearrange("p (m c) -> p m c", m=R)
-                    queue.dma_start(dst[:, m0:m1, e0 * U : e1 * U], st[:, half, :, :])
+                layer2_half(e, half, bank[:, half * C : (half + 1) * C], slice(0, C))
+            copy_out(
+                stage[g][:, :, :, (e - e0) * U : (e - e0 + 1) * U],
+                bank[:].rearrange("p (h m u) -> p h m u", h=2, u=U),
+            )
+            if e == e1 - 1:
+                for half in range(2):
+                    nc.sync.dma_start(out_rows(half)[:, :, e0 * U : e1 * U], stage[g][:, half, :, :])
 
-        def finish_last():
+        def layer2_last(j, two_banks, copies, queues):
             e = E - 1
-            codes = ring.tile([P, P], U32, name="codes", align_bytes=64)
-            scales = ring.tile([P, P], U8, name="scales", align_bytes=64)
-            nc.vector.quantize_mx(out=codes[:].bitcast(FP8X4), scales=scales[:], in_=hq[e, 1][:])
-            st = stage[e, 1][1]
-            for half, copy_out, queue in ((0, nc.vector.tensor_copy, nc.sync), (1, nc.scalar.copy, nc.scalar)):
-                y = ps_a.tile([P, P], F32, name="acc")
-                nc.tensor.matmul_mx(
-                    out=y[:],
-                    lhsT=w2w[:, e, 2 * P * half : 2 * P * (half + 1)].bitcast(FP4X4),
-                    lhsT_scale=w2s[:, e, P * half : P * (half + 1)],
-                    rhs=codes[:].bitcast(FP8X4),
-                    rhs_scale=scales[:],
-                    start=True,
-                    stop=True,
-                )
-                copy_out(st[:, half, :, :], y[:].rearrange("p (m u) -> p m u", u=U))
-                dst = out[P * half : P * (half + 1), :].rearrange("p (m c) -> p m c", m=R)
-                queue.dma_start(dst[:, 2:4, e * U : E * U], st[:, half, :, :])
+            for half in range(2):
+                y = two_banks[half][:, half * P : (half + 1) * P]
+                layer2_half(e, half, y, slice(j * P, (j + 1) * P))
+                copies[half](last[j][half][:], y.rearrange("p (m u) -> p m u", u=U))
+                queues[half].dma_start(out_rows(half)[:, 2 * j : 2 * j + 2, e * U : E * U], last[j][half][:])
 
-        for e0, e1, m0, m1 in [(0, 2, 0, 4), (2, 4, 0, 4), (4, 6, 0, 4), (6, 7, 0, 4), (7, 8, 0, 2), (7, 8, 2, 4)]:
-            st_tile = keep.tile([P, 2, m1 - m0, (e1 - e0) * U], F32, name=f"stage{e0}_{m0}")
-            for e in range(e0, e1):
-                stage[e, m0 // 2] = (e0, st_tile)
-            stores[e1 - 1, m0 // 2] = (e1, m0, m1)
+        def flat(tile):
+            return tile[:].rearrange("p g i -> p (g i)")
 
-        w1s_flat = w1s[:].rearrange("p g i -> p (g i)")
-        nc.gpsimd.memset(xs[:].bitcast(I32), 0)
         nc.sync.dma_start(lists[:], offs)
-        load_x_words(0)
-        for q, queue in enumerate((nc.scalar, nc.sync, nc.scalar, nc.sync)):
-            queue.dma_start(xs[32 * q : 32 * q + 12, :T].bitcast(I32), x_scales[:, 4 * q : 4 * q + 4, :].bitcast(I32))
-        zero(w1s_flat[:, : 3 * PASSES * H], nc.vector)
+        zero(xs[:], nc.vector)
+        load_xs_pass0(0, nc.sync)
+        load_xs_pass0(1, nc.sync)
+        load_xs_rest(0, nc.scalar)
+        load_xs_rest(1, nc.scalar)
+        load_xs_pass0(2, nc.sync)
+        load_xs_pass0(3, nc.scalar)
+        nc.sync.dma_start(xw01[:], x_words[0:2].rearrange("a p t r -> p a (t r)").bitcast(I32))
+        zero(flat(w1s[0]), nc.vector)
+        zero(flat(w1s[1]), nc.vector)
         make_identity(nc, ident[:])
-        load_w1_scales(0, 3, (nc.scalar, nc.scalar, nc.scalar, nc.scalar))
-        load_w1_words(0, 1)
-        load_x_words(1)
-        load_x_words(2)
-        nc.vector.memset(warm[:, 0:1], 0.0)
-        nc.scalar.activation(warm[:, 8:9], warm[:, 0:1], GELU)
-        for plane in moved:
-            zero(plane[:], nc.vector)
-        gather_scales(0, (nc.scalar, nc.scalar))
-        load_w1_words(1, 2)
-        zero(w1s_flat[:, 3 * PASSES * H :], nc.vector)
-        zero(w2s[:].rearrange("p e n -> p (e n)"), nc.vector)
-        gather_expert(0, 0, C)
-        gather_scales(1, (nc.scalar, nc.scalar))
-        load_w1_scales(3, 5, (nc.scalar, nc.sync, nc.scalar, nc.sync))
-        load_w1_words(2, 3)
-        load_w2_scales((nc.scalar, nc.sync, nc.scalar, nc.sync))
-        load_w1_words(3, 5)
-        load_w2_words(0, 4, nc.sync)
-        layer1(0, (0, 1))
-        gather_expert(1, 0, C)
-        load_w1_scales(5, E, (nc.sync, nc.sync, nc.sync, nc.sync))
-        load_w1_words(5, 8)
-        load_w2_words(4, E, nc.sync)
-        layer1(1, (0, 1))
-        turn(0, (0, 1), nc.scalar.copy)
-        gather_expert(2, 0, C)
-        layer1(2, (0, 1))
-        turn(1, (0, 1), nc.scalar.copy)
-        gather_expert(3, 0, C)
-        gather_scales(2, (nc.sync, nc.sync))
-        layer1(3, (0, 1))
-        turn(2, (0, 1), nc.scalar.copy)
-        finish(0, (0, 1), nc.scalar.copy)
-        gather_expert(4, 0, C)
-        layer1(4, (0, 1))
-        turn(3, (0, 1), nc.scalar.copy)
-        finish(1, (0, 1), nc.scalar.copy)
-        gather_expert(5, 0, C)
-        layer1(5, (0, 1))
-        turn(4, (0, 1), nc.scalar.copy)
-        finish(2, (0, 1), nc.scalar.copy)
-        finish(3, (0, 1), nc.scalar.copy)
-        gather_expert(6, 0, C)
-        layer1(6, (0, 1))
-        turn(5, (0, 1), nc.vector.tensor_copy)
-        finish(4, (0, 1), nc.scalar.copy)
-        gather_expert(7, 0, P)
-        layer1(7, (0,))
-        turn(6, (0, 1), nc.vector.tensor_copy)
-        finish(5, (0, 1), nc.vector.tensor_copy)
-        gather_expert(7, P, C)
-        layer1(7, (1,))
-        turn(7, (0,), nc.scalar.copy)
-        finish(6, (0, 1), nc.vector.tensor_copy)
-        finish(7, (0,), nc.scalar.copy)
-        turn(7, (1,), nc.scalar.copy)
-        finish_last()
+        zero(flat(w2s), nc.gpsimd)
+        zero(flat(w1s[2]), nc.gpsimd)
+        zero(flat(w1s[3]), nc.gpsimd)
+        load_w1_words(0)
+        load_w1_scales(0)
+        nc.sync.dma_start(xw2[:], x_words[2].rearrange("p t r -> p (t r)").bitcast(I32))
+        gather_scales(0)
+        load_w1_words(1)
+        load_w1_scales(1)
+        load_w1_words(2)
+        load_w1_words(3)
+        gather_words(0)
+        gather_words(1)
+
+        on_scalar, on_vector = nc.scalar.copy, nc.vector.tensor_copy
+        for e in range(E - 1):
+            layer1(e, 0)
+            if e == 1:
+                gather_scales(1)
+                load_w1_scales(2)
+                load_w1_words(4)
+                load_w1_words(5)
+                load_w1_scales(3)
+                load_w1_words(6)
+            if e >= 3:
+                layer2(e - 3, acc_bank(e - 1, 1), on_scalar)
+            layer1(e, 1)
+            if e == 0:
+                load_w2_scales(nc.sync)
+                nc.sync.dma_start(w2w[:].bitcast(I32), w2_words.rearrange("e s p b -> p (e s) b").bitcast(I32))
+            if e == 3:
+                gather_scales(2)
+            if e + 2 < E:
+                gather_words(e + 2)
+            if e >= 1:
+                turn(e - 1, acc_bank(e, 0), on_scalar)
+        layer1(7, 0)
+        layer2(4, acc_bank(6, 1), on_scalar)
+        turn(6, banks[4], on_vector)
+        layer1(7, 1)
+        layer2(5, banks[5], on_vector)
+        turn(7, banks[6], on_vector, js=(0,))
+        turn(7, banks[7], on_scalar, js=(1,))
+        layer2(6, banks[0], on_scalar)
+        layer2_last(0, (banks[1], banks[1]), (on_vector, on_vector), (nc.sync, nc.sync))
+        layer2_last(1, (banks[2], banks[4]), (on_vector, on_scalar), (nc.sync, nc.scalar))

@@ -24,7 +24,7 @@ CUTS = (0, 3, 6, 8)
 WINDOW = 1024
 W1_WORD_GROUPS = ((0, 1), (1, 2), (2, 3), (3, 4), (4, 5), (5, 6), (6, 8))
 W1_SCALE_GROUPS = ((0, 2), (2, 4), (4, 6), (6, 8))
-STORE_GROUPS = ((0, 2), (2, 4), (4, 6), (6, 7))
+STORE_GROUPS = ((0, 2), (2, 4), (4, 6), (6, 8))
 
 
 def tile_moe_pke_mlp_gelu_kernel(
@@ -54,11 +54,10 @@ def tile_moe_pke_mlp_gelu_kernel(
         moved = [sbuf([P, S], U8, f"moved{a}") for a in (1, 2)]
         ident = sbuf([P, P], F32, "ident")
         hb = {(e, j): sbuf([P, H], BF16, f"h{e}_{j}") for e in range(E) for j in range(2)}
-        ht = [sbuf([P, 4 * C], BF16, f"ht{e}") for e in range(E)]
-        codes = [sbuf([P, C], U32, f"codes{e}") for e in range(E)]
-        scales = [sbuf([P, C], U8, f"scales{e}") for e in range(E)]
+        ht = sbuf([P, 4 * S], BF16, "ht")
+        codes = sbuf([P, S], U32, "codes")
+        scales = sbuf([P, S], U8, "scales")
         stage = [keep.tile([P, 2, R, (e1 - e0) * U], F32, name=f"stage{e0}") for e0, e1 in STORE_GROUPS]
-        last = [[keep.tile([P, 2, U], F32, name=f"last{j}_{half}") for half in range(2)] for j in range(2)]
 
         def group_of(groups, e):
             return [g for g, (e0, e1) in enumerate(groups) if e0 <= e < e1][0]
@@ -133,33 +132,43 @@ def tile_moe_pke_mlp_gelu_kernel(
                     start=(a == pass_order(e)[0]),
                     stop=(a == pass_order(e)[-1]),
                 )
-            nc.scalar.activation(
-                hb[e, j][:].rearrange("s (u p t) -> s u p t", u=2, t=2),
-                acc[:].rearrange("s (p u t) -> s u p t", u=2, t=2),
-                GELU,
-            )
+            h_view = hb[e, j][:].rearrange("s (u p t) -> s u p t", u=2, t=2)
+            acc_view = acc[:].rearrange("s (p u t) -> s u p t", u=2, t=2)
+            for u0, u1 in ((0, 1), (1, 2)) if (j == 0 and e > 0) or e == E - 1 else ((0, 2),):
+                nc.scalar.activation(h_view[:, u0:u1], acc_view[:, u0:u1], GELU)
 
-        def turn(e, bank, copy_out, js=(0, 1)):
-            cols = slice(js[0] * P, (js[-1] + 1) * P)
-            xt = bank[:, : 2 * P * len(js)].rearrange("p (j u s) -> p j u s", u=2, s=P)
-            for i, j in enumerate(js):
-                pairs = hb[e, j][:].bitcast(F32)
-                for u in range(2):
-                    nc.tensor.transpose(xt[:, i, u, :], pairs[:, u * P : (u + 1) * P], ident[:])
-            words = ht[e][:, 4 * cols.start : 4 * cols.stop]
+        def turn(t0, t1, bank):
+            xt = bank[:, : 2 * P * (t1 - t0)].rearrange("p (j u s) -> p j u s", u=2, s=P)
+            newest = t1 - 1
+            order = [(newest, 0)] + [(t, u) for t in range(t0, newest) for u in range(2)] + [(newest, 1)]
+            for t, u in order:
+                pairs = hb[t // 2, t % 2][:].bitcast(F32)
+                nc.tensor.transpose(xt[:, t - t0, u, :], pairs[:, u * P : (u + 1) * P], ident[:])
+
+        def quantise(t0, t1, bank, copy_out):
+            xt = bank[:, : 2 * P * (t1 - t0)].rearrange("p (j u s) -> p j u s", u=2, s=P)
+            cols = slice(t0 * P, t1 * P)
+            words = ht[:, 4 * cols.start : 4 * cols.stop]
             copy_out(
                 words.bitcast(F32).rearrange("p (j s u) -> p j s u", s=P, u=2),
                 xt.rearrange("p j u s -> p j s u"),
             )
-            nc.vector.quantize_mx(out=codes[e][:, cols].bitcast(FP8X4), scales=scales[e][:, cols], in_=words)
+            nc.vector.quantize_mx(out=codes[:, cols].bitcast(FP8X4), scales=scales[:, cols], in_=words)
+
+        def turn_run(pieces):
+            for t0, t1, bank, copy_out in pieces:
+                turn(t0, t1, bank)
+            for t0, t1, bank, copy_out in pieces:
+                quantise(t0, t1, bank, copy_out)
 
         def layer2_half(e, half, y, cols):
+            slots = slice(e * C + cols.start, e * C + cols.stop)
             nc.tensor.matmul_mx(
                 out=y,
                 lhsT=w2w[:, e, 2 * P * half : 2 * P * (half + 1)].bitcast(FP4X4),
                 lhsT_scale=w2s[:, e, P * half : P * (half + 1)],
-                rhs=codes[e][:, cols].bitcast(FP8X4),
-                rhs_scale=scales[e][:, cols],
+                rhs=codes[:, slots].bitcast(FP8X4),
+                rhs_scale=scales[:, slots],
                 start=True,
                 stop=True,
             )
@@ -185,14 +194,15 @@ def tile_moe_pke_mlp_gelu_kernel(
             for half in range(2):
                 y = two_banks[half][:, half * P : (half + 1) * P]
                 layer2_half(e, half, y, slice(j * P, (j + 1) * P))
-                copies[half](last[j][half][:], y.rearrange("p (m u) -> p m u", u=U))
-                queues[half].dma_start(out_rows(half)[:, 2 * j : 2 * j + 2, e * U : E * U], last[j][half][:])
+                ranks = slice(2 * j, 2 * j + 2)
+                copies[half](stage[-1][:, half, ranks, U:], y.rearrange("p (m u) -> p m u", u=U))
+                queues[half].dma_start(out_rows(half)[:, ranks, (e - 1) * U : E * U], stage[-1][:, half, ranks, :])
 
         def flat(tile):
             return tile[:].rearrange("p g i -> p (g i)")
 
         nc.sync.dma_start(lists[:], offs)
-        zero(xs[:], nc.vector)
+        zero(xs[:, :T], nc.vector)
         load_xs_pass0(0, nc.sync)
         load_xs_pass0(1, nc.sync)
         load_xs_rest(0, nc.scalar)
@@ -200,6 +210,7 @@ def tile_moe_pke_mlp_gelu_kernel(
         load_xs_pass0(2, nc.sync)
         load_xs_pass0(3, nc.scalar)
         nc.sync.dma_start(xw01[:], x_words[0:2].rearrange("a p t r -> p a (t r)").bitcast(I32))
+        zero(xs[:, T:], nc.vector)
         zero(flat(w1s[0]), nc.vector)
         zero(flat(w1s[1]), nc.vector)
         make_identity(nc, ident[:])
@@ -218,7 +229,7 @@ def tile_moe_pke_mlp_gelu_kernel(
         gather_words(1)
 
         on_scalar, on_vector = nc.scalar.copy, nc.vector.tensor_copy
-        for e in range(E - 1):
+        for e in range(E):
             layer1(e, 0)
             if e == 1:
                 gather_scales(1)
@@ -227,8 +238,6 @@ def tile_moe_pke_mlp_gelu_kernel(
                 load_w1_words(5)
                 load_w1_scales(3)
                 load_w1_words(6)
-            if e >= 3:
-                layer2(e - 3, acc_bank(e - 1, 1), on_scalar)
             layer1(e, 1)
             if e == 0:
                 load_w2_scales(nc.sync)
@@ -237,15 +246,18 @@ def tile_moe_pke_mlp_gelu_kernel(
                 gather_scales(2)
             if e + 2 < E:
                 gather_words(e + 2)
-            if e >= 1:
-                turn(e - 1, acc_bank(e, 0), on_scalar)
-        layer1(7, 0)
-        layer2(4, acc_bank(6, 1), on_scalar)
-        turn(6, banks[4], on_vector)
-        layer1(7, 1)
-        layer2(5, banks[5], on_vector)
-        turn(7, banks[6], on_vector, js=(0,))
-        turn(7, banks[7], on_scalar, js=(1,))
-        layer2(6, banks[0], on_scalar)
-        layer2_last(0, (banks[1], banks[1]), (on_vector, on_vector), (nc.sync, nc.sync))
-        layer2_last(1, (banks[2], banks[4]), (on_vector, on_scalar), (nc.sync, nc.scalar))
+            if e == 1:
+                turn_run([(1, 3, banks[5], on_scalar), (0, 1, acc_bank(1, 0), on_scalar)])
+            if e >= 2:
+                turn_run([(2 * e - 1, 2 * e + 1, banks[4 + e % 2], on_vector if e == E - 1 else on_scalar)])
+            if e in (3, 4):
+                layer2(e - 3, acc_bank(e, 0), on_scalar)
+            if e == 5:
+                layer2(2, acc_bank(e, 0), on_scalar)
+                layer2(3, acc_bank(e, 1), on_vector)
+            if e >= 6:
+                layer2(e - 2, acc_bank(e, 0), on_vector if e == 6 else on_scalar)
+        turn_run([(15, 16, banks[6], on_scalar)])
+        layer2(6, banks[7], on_scalar)
+        layer2_last(0, (banks[0], banks[0]), (on_vector, on_vector), (nc.sync, nc.sync))
+        layer2_last(1, (banks[1], banks[4]), (on_vector, on_scalar), (nc.sync, nc.scalar))

@@ -20,11 +20,11 @@ P = 128
 PASSES = K // 512
 S = E * C
 U = C // R
-CUTS = (0, 3, 6, 8)
-WINDOW = 1024
+CUTS = (0, 4, 6, 8)
+WINDOW = 1408
 W1_WORD_GROUPS = ((0, 1), (1, 2), (2, 3), (3, 4), (4, 5), (5, 6), (6, 8))
 W1_SCALE_GROUPS = ((0, 2), (2, 4), (4, 6), (6, 8))
-STORE_GROUPS = ((0, 2), (2, 4), (4, 6), (6, 8))
+STORE_GROUPS = ((0, 2), (2, 5), (5, 6), (6, 8))
 
 
 def tile_moe_pke_mlp_gelu_kernel(
@@ -45,12 +45,12 @@ def tile_moe_pke_mlp_gelu_kernel(
         xw2 = sbuf([P, T], I32, "xw2")
         windows = [xw01[:, 0, :], xw01[:, 1, :], xw2[:]]
         w1w = [sbuf([P, (e1 - e0) * PASSES, 2 * H], U8, f"w1w{e0}") for e0, e1 in W1_WORD_GROUPS]
-        w1s = [sbuf([P, (e1 - e0) * PASSES, H], U8, f"w1s{e0}") for e0, e1 in W1_SCALE_GROUPS]
+        w1s = 2 * [sbuf([P, 2 * PASSES, H], U8, f"w1s{g}") for g in range(2)]
         w2w = sbuf([P, E, 2 * N], U8, "w2w")
         w2s = sbuf([P, E, N], U8, "w2s")
         gw = [[sbuf([P, C], U32, f"gw{s}_{a}") for a in range(PASSES)] for s in range(2)]
         gs = sbuf([P, 6 * C - P], U8, "gs")
-        gs_start = (3 * C - P, C, 0)
+        gs_start = (0, P, 4 * C - P)
         moved = [sbuf([P, S], U8, f"moved{a}") for a in (1, 2)]
         ident = sbuf([P, P], F32, "ident")
         hb = {(e, j): sbuf([P, H], BF16, f"h{e}_{j}") for e in range(E) for j in range(2)}
@@ -62,8 +62,8 @@ def tile_moe_pke_mlp_gelu_kernel(
         def group_of(groups, e):
             return [g for g, (e0, e1) in enumerate(groups) if e0 <= e < e1][0]
 
-        def zero(ap, engine):
-            engine.memset(ap.bitcast(I32), 0)
+        def zero(ap):
+            nc.vector.memset(ap.bitcast(I32), 0)
 
         def load_xs_pass0(quad, queue):
             queue.dma_start(xs[32 * quad : 32 * quad + 4, :T].bitcast(I32), x_scales[0, 4 * quad : 4 * quad + 4, :].bitcast(I32))
@@ -94,8 +94,8 @@ def tile_moe_pke_mlp_gelu_kernel(
             return (0, 1, 2) if e < 2 else (2, 1, 0)
 
         def gather_words(e):
-            for a in pass_order(e):
-                nc.vector.tensor_copy(gw[e % 2][a][:], windows[a].bitcast(U32).indirect(offsets(e * C, (e + 1) * C)))
+            for i, a in enumerate(pass_order(e)):
+                nc.vector.tensor_copy(gw[e % 2][i][:], windows[a].bitcast(U32).indirect(offsets(e * C, (e + 1) * C)))
 
         def gather_scales(c):
             s0, s1 = C * CUTS[c], C * CUTS[c + 1]
@@ -122,15 +122,15 @@ def tile_moe_pke_mlp_gelu_kernel(
         def layer1(e, j):
             gwords, gscales = group_of(W1_WORD_GROUPS, e), group_of(W1_SCALE_GROUPS, e)
             acc = acc_bank(e, j)
-            for a in pass_order(e):
+            for i, a in enumerate(pass_order(e)):
                 nc.tensor.matmul_mx(
                     out=acc[:],
-                    lhsT=gw[e % 2][a][:, j * P : (j + 1) * P].bitcast(FP8X4),
+                    lhsT=gw[e % 2][i][:, j * P : (j + 1) * P].bitcast(FP8X4),
                     lhsT_scale=x_plane(a, e * C + j * P),
                     rhs=w1w[gwords][:, (e - W1_WORD_GROUPS[gwords][0]) * PASSES + a, :].bitcast(FP4X4),
                     rhs_scale=w1s[gscales][:, (e - W1_SCALE_GROUPS[gscales][0]) * PASSES + a, :],
-                    start=(a == pass_order(e)[0]),
-                    stop=(a == pass_order(e)[-1]),
+                    start=(i == 0),
+                    stop=(i == PASSES - 1),
                 )
             h_view = hb[e, j][:].rearrange("s (u p t) -> s u p t", u=2, t=2)
             acc_view = acc[:].rearrange("s (p u t) -> s u p t", u=2, t=2)
@@ -202,7 +202,7 @@ def tile_moe_pke_mlp_gelu_kernel(
             return tile[:].rearrange("p g i -> p (g i)")
 
         nc.sync.dma_start(lists[:], offs)
-        zero(xs[:, :T], nc.vector)
+        zero(xs[:, :T])
         load_xs_pass0(0, nc.sync)
         load_xs_pass0(1, nc.sync)
         load_xs_rest(0, nc.scalar)
@@ -210,13 +210,12 @@ def tile_moe_pke_mlp_gelu_kernel(
         load_xs_pass0(2, nc.sync)
         load_xs_pass0(3, nc.scalar)
         nc.sync.dma_start(xw01[:], x_words[0:2].rearrange("a p t r -> p a (t r)").bitcast(I32))
-        zero(xs[:, T:], nc.vector)
-        zero(flat(w1s[0]), nc.vector)
-        zero(flat(w1s[1]), nc.vector)
-        make_identity(nc, ident[:])
-        zero(flat(w2s), nc.gpsimd)
-        zero(flat(w1s[2]), nc.gpsimd)
-        zero(flat(w1s[3]), nc.gpsimd)
+        nc.vector.memset(ident[:], 0.0)
+        make_identity(nc, ident[:], nomemset=True)
+        zero(flat(w1s[0]))
+        zero(xs[:, T:])
+        zero(flat(w1s[1]))
+        zero(flat(w2s))
         load_w1_words(0)
         load_w1_scales(0)
         nc.sync.dma_start(xw2[:], x_words[2].rearrange("p t r -> p (t r)").bitcast(I32))
@@ -231,19 +230,20 @@ def tile_moe_pke_mlp_gelu_kernel(
         on_scalar, on_vector = nc.scalar.copy, nc.vector.tensor_copy
         for e in range(E):
             layer1(e, 0)
-            if e == 1:
+            if e == 2:
                 gather_scales(1)
-                load_w1_scales(2)
-                load_w1_words(4)
-                load_w1_words(5)
-                load_w1_scales(3)
                 load_w1_words(6)
             layer1(e, 1)
             if e == 0:
                 load_w2_scales(nc.sync)
                 nc.sync.dma_start(w2w[:].bitcast(I32), w2_words.rearrange("e s p b -> p (e s) b").bitcast(I32))
+                load_w1_words(4)
+                load_w1_words(5)
+            if e == 1:
+                load_w1_scales(2)
             if e == 3:
                 gather_scales(2)
+                load_w1_scales(3)
             if e + 2 < E:
                 gather_words(e + 2)
             if e == 1:

@@ -24,7 +24,7 @@ CUTS = (0, 4, 6, 8)
 WINDOW = 1408
 W1_WORD_GROUPS = ((0, 1), (1, 2), (2, 3), (3, 4), (4, 5), (5, 6), (6, 8))
 W1_SCALE_GROUPS = ((0, 2), (2, 4), (4, 6), (6, 8))
-STORE_GROUPS = ((0, 2), (2, 5), (5, 6), (6, 8))
+STORE_GROUPS = ((0, 2), (2, 4), (4, 6), (6, 8))
 
 
 def tile_moe_pke_mlp_gelu_kernel(
@@ -94,8 +94,10 @@ def tile_moe_pke_mlp_gelu_kernel(
             return (0, 1, 2) if e < 2 else (2, 1, 0)
 
         def gather_words(e):
-            for i, a in enumerate(pass_order(e)):
-                nc.vector.tensor_copy(gw[e % 2][i][:], windows[a].bitcast(U32).indirect(offsets(e * C, (e + 1) * C)))
+            for c0, c1 in ((0, P), (P, C)) if e == E - 1 else ((0, C),):
+                for i, a in enumerate(pass_order(e)):
+                    picked = windows[a].bitcast(U32).indirect(offsets(e * C + c0, e * C + c1))
+                    nc.vector.tensor_copy(gw[e % 2][i][:, c0:c1], picked)
 
         def gather_scales(c):
             s0, s1 = C * CUTS[c], C * CUTS[c + 1]
@@ -250,14 +252,10 @@ def tile_moe_pke_mlp_gelu_kernel(
                 turn_run([(1, 3, banks[5], on_scalar), (0, 1, acc_bank(1, 0), on_scalar)])
             if e >= 2:
                 turn_run([(2 * e - 1, 2 * e + 1, banks[4 + e % 2], on_vector if e == E - 1 else on_scalar)])
-            if e in (3, 4):
+            if e >= 3:
                 layer2(e - 3, acc_bank(e, 0), on_scalar)
-            if e == 5:
-                layer2(2, acc_bank(e, 0), on_scalar)
-                layer2(3, acc_bank(e, 1), on_vector)
-            if e >= 6:
-                layer2(e - 2, acc_bank(e, 0), on_vector if e == 6 else on_scalar)
+        layer2(5, banks[1], on_vector)
         turn_run([(15, 16, banks[6], on_scalar)])
         layer2(6, banks[7], on_scalar)
         layer2_last(0, (banks[0], banks[0]), (on_vector, on_vector), (nc.sync, nc.sync))
-        layer2_last(1, (banks[1], banks[4]), (on_vector, on_scalar), (nc.sync, nc.scalar))
+        layer2_last(1, (banks[3], banks[4]), (on_vector, on_scalar), (nc.sync, nc.scalar))

@@ -74,14 +74,14 @@ def tile_moe_pke_mlp_gelu_kernel(
 
         def load_w1_scales(g):
             e0, e1 = W1_SCALE_GROUPS[g]
-            src = w1_scales[e0:e1].rearrange("e s q i -> q (e s) i")
-            for q in (0, 2, 1, 3):
-                nc.sync.dma_start(w1s[g][32 * q : 32 * q + 4].bitcast(I32), src[4 * q : 4 * q + 4].bitcast(I32))
+            src = w1_scales[e0:e1].rearrange("e s (q r) i -> r q (e s) i", r=4)
+            for r in range(4):
+                nc.sync.dma_start(w1s[g][r:P:32].bitcast(I32), src[r].bitcast(I32))
 
         def load_w2_scales(queue):
-            src = w2_scales.rearrange("e s q n -> q (e s) n")
-            for q in (0, 2, 1, 3):
-                queue.dma_start(w2s[32 * q : 32 * q + 4].bitcast(I32), src[4 * q : 4 * q + 4].bitcast(I32))
+            src = w2_scales.rearrange("e s (q r) n -> r q (e s) n", r=4)
+            for r in range(4):
+                queue.dma_start(w2s[r:P:32].bitcast(I32), src[r].bitcast(I32))
 
         def load_w1_words(g):
             e0, e1 = W1_WORD_GROUPS[g]
@@ -234,15 +234,15 @@ def tile_moe_pke_mlp_gelu_kernel(
             layer1(e, 0)
             if e == 2:
                 gather_scales(1)
+                load_w1_words(5)
                 load_w1_words(6)
             layer1(e, 1)
             if e == 0:
                 load_w2_scales(nc.sync)
                 nc.sync.dma_start(w2w[:].bitcast(I32), w2_words.rearrange("e s p b -> p (e s) b").bitcast(I32))
-                load_w1_words(4)
-                load_w1_words(5)
             if e == 1:
                 load_w1_scales(2)
+                load_w1_words(4)
             if e == 3:
                 gather_scales(2)
                 load_w1_scales(3)

@@ -20,11 +20,14 @@ P = 128
 PASSES = K // 512
 S = E * C
 U = C // R
-CUTS = (0, 4, 6, 8)
+LAST = E - 1
+LAG = 3
+
+SCALE_GATHERS = ((0, 4), (4, 6), (6, 8))
 WINDOW = 1408
 W1_WORD_GROUPS = ((0, 1), (1, 2), (2, 3), (3, 4), (4, 5), (5, 6), (6, 8))
-W1_SCALE_GROUPS = ((0, 2), (2, 4), (4, 6), (6, 8))
-STORE_GROUPS = ((0, 2), (2, 4), (4, 6), (6, 8))
+W1_SCALE_GROUPS = ((0, 1), (1, 3), (3, 5), (5, 7), (7, 8))
+STORE_GROUPS = ((0, 3), (3, 5), (5, 6), (6, 8))
 
 
 def tile_moe_pke_mlp_gelu_kernel(
@@ -40,23 +43,24 @@ def tile_moe_pke_mlp_gelu_kernel(
 
         banks = [psum.tile([P, 512], F32, name=f"bank{b}") for b in range(8)]
         lists = keep.tile([P, S // 16], U16, name="lists")
-        xs = sbuf([P, WINDOW], U8, "xs")
-        xw01 = sbuf([P, 2, T], I32, "xw01")
-        xw2 = sbuf([P, T], I32, "xw2")
-        windows = [xw01[:, 0, :], xw01[:, 1, :], xw2[:]]
+        x_scale_window = sbuf([P, WINDOW], U8, "x_scale_window")
+        x_words01 = sbuf([P, 2, T], I32, "x_words01")
+        x_words2 = sbuf([P, T], I32, "x_words2")
+        word_windows = [x_words01[:, 0, :], x_words01[:, 1, :], x_words2[:]]
         w1w = [sbuf([P, (e1 - e0) * PASSES, 2 * H], U8, f"w1w{e0}") for e0, e1 in W1_WORD_GROUPS]
-        w1s = 2 * [sbuf([P, 2 * PASSES, H], U8, f"w1s{g}") for g in range(2)]
+        w1s_tiles = [sbuf([P, (e1 - e0) * PASSES, H], U8, f"w1s{e0}") for e0, e1 in W1_SCALE_GROUPS[:3]]
+        w1s = w1s_tiles + [w1s_tiles[1], w1s_tiles[0]]
         w2w = sbuf([P, E, 2 * N], U8, "w2w")
         w2s = sbuf([P, E, N], U8, "w2s")
-        gw = [[sbuf([P, C], U32, f"gw{s}_{a}") for a in range(PASSES)] for s in range(2)]
-        gs = sbuf([P, 6 * C - P], U8, "gs")
-        gs_start = (0, P, 4 * C - P)
-        moved = [sbuf([P, S], U8, f"moved{a}") for a in (1, 2)]
+        picked_words = [[sbuf([P, C], U32, f"picked_words{s}_{i}") for i in range(PASSES)] for s in range(2)]
+        picked_scales = sbuf([P, 6 * C - P], U8, "picked_scales")
+        picked_scales_start = (0, P, 4 * C - P)
+        moved_planes = [sbuf([P, S], U8, f"moved_plane{a}") for a in (1, 2)]
         ident = sbuf([P, P], F32, "ident")
-        hb = {(e, j): sbuf([P, H], BF16, f"h{e}_{j}") for e in range(E) for j in range(2)}
-        ht = sbuf([P, 4 * S], BF16, "ht")
-        codes = sbuf([P, S], U32, "codes")
-        scales = sbuf([P, S], U8, "scales")
+        h_pairs = [sbuf([P, H], BF16, f"h_pairs{t}") for t in range(2 * E)]
+        h_turned = sbuf([P, 4 * S], BF16, "h_turned")
+        h_codes = sbuf([P, S], U32, "h_codes")
+        h_scales = sbuf([P, S], U8, "h_scales")
         stage = [keep.tile([P, 2, R, (e1 - e0) * U], F32, name=f"stage{e0}") for e0, e1 in STORE_GROUPS]
 
         def group_of(groups, e):
@@ -65,23 +69,28 @@ def tile_moe_pke_mlp_gelu_kernel(
         def zero(ap):
             nc.vector.memset(ap.bitcast(I32), 0)
 
-        def load_xs_pass0(quad, queue):
-            queue.dma_start(xs[32 * quad : 32 * quad + 4, :T].bitcast(I32), x_scales[0, 4 * quad : 4 * quad + 4, :].bitcast(I32))
+        def flat(tile):
+            return tile[:].rearrange("p g i -> p (g i)")
 
-        def load_xs_rest(q, queue):
-            src = x_scales.rearrange("a (h q r) t -> (a h) q r t", h=2, q=2)
-            queue.dma_start(xs[32 * q + 4 : 32 * q + 20, :T].bitcast(I32), src[2:6, q].bitcast(I32))
+        def load_x_scales_pass0(quadrant, queue):
+            rows = x_scales[0, 4 * quadrant : 4 * quadrant + 4, :]
+            queue.dma_start(x_scale_window[32 * quadrant : 32 * quadrant + 4, :T].bitcast(I32), rows.bitcast(I32))
+
+        def load_x_scales_passes12(q, queue):
+            rows = x_scales.rearrange("a (h q r) t -> (a h) q r t", h=2, q=2)[2:6, q]
+            queue.dma_start(x_scale_window[32 * q + 4 : 32 * q + 20, :T].bitcast(I32), rows.bitcast(I32))
 
         def load_w1_scales(g):
             e0, e1 = W1_SCALE_GROUPS[g]
-            src = w1_scales[e0:e1].rearrange("e s (q r) i -> r q (e s) i", r=4)
+            rows = w1_scales[e0:e1].rearrange("e s (q r) i -> r q (e s) i", r=4)
             for r in range(4):
-                nc.sync.dma_start(w1s[g][r:P:32].bitcast(I32), src[r].bitcast(I32))
+                nc.sync.dma_start(w1s[g][r:P:32].bitcast(I32), rows[r].bitcast(I32))
 
-        def load_w2_scales(queue):
-            src = w2_scales.rearrange("e s (q r) n -> r q (e s) n", r=4)
+        def load_w2():
+            rows = w2_scales.rearrange("e s (q r) n -> r q (e s) n", r=4)
             for r in range(4):
-                queue.dma_start(w2s[r:P:32].bitcast(I32), src[r].bitcast(I32))
+                nc.sync.dma_start(w2s[r:P:32].bitcast(I32), rows[r].bitcast(I32))
+            nc.sync.dma_start(w2w[:].bitcast(I32), w2_words.rearrange("e s p b -> p (e s) b").bitcast(I32))
 
         def load_w1_words(g):
             e0, e1 = W1_WORD_GROUPS[g]
@@ -91,86 +100,91 @@ def tile_moe_pke_mlp_gelu_kernel(
             return lists[:, s0 // 16 : s1 // 16]
 
         def pass_order(e):
-            return (0, 1, 2) if e < 2 else (2, 1, 0)
+            return (0, 1, 2) if e == 0 else (2, 1, 0)
 
-        def gather_words(e):
-            for c0, c1 in ((0, P), (P, C)) if e == E - 1 else ((0, C),):
-                for i, a in enumerate(pass_order(e)):
-                    picked = windows[a].bitcast(U32).indirect(offsets(e * C + c0, e * C + c1))
-                    nc.vector.tensor_copy(gw[e % 2][i][:, c0:c1], picked)
+        def word_buffers(e, j):
+            return picked_words[0] if (e, j) == (LAST, 1) else picked_words[e % 2]
 
-        def gather_scales(c):
-            s0, s1 = C * CUTS[c], C * CUTS[c + 1]
-            cols = slice(gs_start[c], gs_start[c] + s1 - s0)
-            nc.vector.tensor_copy(gs[:, cols], xs[:].indirect(offsets(s0, s1)))
+        def gather_words(e, c0=0, c1=C):
+            for i, a in enumerate(pass_order(e)):
+                picked = word_windows[a].bitcast(U32).indirect(offsets(e * C + c0, e * C + c1))
+                nc.vector.tensor_copy(word_buffers(e, c0 // P)[i][:, c0:c1], picked)
+
+        def gather_scales(g):
+            e0, e1 = SCALE_GATHERS[g]
+            s0, s1 = e0 * C, e1 * C
+            cols = slice(picked_scales_start[g], picked_scales_start[g] + s1 - s0)
+            nc.vector.tensor_copy(picked_scales[:, cols], x_scale_window[:].indirect(offsets(s0, s1)))
             for a in (1, 2):
                 for h in range(2):
                     row = 4 + 8 * (a - 1) + 4 * h
                     nc.sync.dma_start(
-                        moved[a - 1][64 * h : 64 * h + 64, s0:s1].bitcast(I32),
-                        gs[row : row + 64, cols].bitcast(I32),
+                        moved_planes[a - 1][64 * h : 64 * h + 64, s0:s1].bitcast(I32),
+                        picked_scales[row : row + 64, cols].bitcast(I32),
                     )
 
-        def x_plane(a, s0):
+        def x_plane(a, e, j):
             if a == 0:
-                c = max(i for i in range(len(CUTS) - 1) if C * CUTS[i] <= s0)
-                c0 = gs_start[c] + s0 - C * CUTS[c]
-                return gs[:, c0 : c0 + P]
-            return moved[a - 1][:, s0 : s0 + P]
+                g = group_of(SCALE_GATHERS, e)
+                c0 = picked_scales_start[g] + (e - SCALE_GATHERS[g][0]) * C + j * P
+                return picked_scales[:, c0 : c0 + P]
+            return moved_planes[a - 1][:, e * C + j * P : e * C + (j + 1) * P]
 
         def acc_bank(e, j):
             return banks[2 * (e % 2) + j]
 
         def layer1(e, j):
-            gwords, gscales = group_of(W1_WORD_GROUPS, e), group_of(W1_SCALE_GROUPS, e)
+            gw, gs = group_of(W1_WORD_GROUPS, e), group_of(W1_SCALE_GROUPS, e)
             acc = acc_bank(e, j)
             for i, a in enumerate(pass_order(e)):
                 nc.tensor.matmul_mx(
                     out=acc[:],
-                    lhsT=gw[e % 2][i][:, j * P : (j + 1) * P].bitcast(FP8X4),
-                    lhsT_scale=x_plane(a, e * C + j * P),
-                    rhs=w1w[gwords][:, (e - W1_WORD_GROUPS[gwords][0]) * PASSES + a, :].bitcast(FP4X4),
-                    rhs_scale=w1s[gscales][:, (e - W1_SCALE_GROUPS[gscales][0]) * PASSES + a, :],
+                    lhsT=word_buffers(e, j)[i][:, j * P : (j + 1) * P].bitcast(FP8X4),
+                    lhsT_scale=x_plane(a, e, j),
+                    rhs=w1w[gw][:, (e - W1_WORD_GROUPS[gw][0]) * PASSES + a, :].bitcast(FP4X4),
+                    rhs_scale=w1s[gs][:, (e - W1_SCALE_GROUPS[gs][0]) * PASSES + a, :],
                     start=(i == 0),
                     stop=(i == PASSES - 1),
                 )
-            h_view = hb[e, j][:].rearrange("s (u p t) -> s u p t", u=2, t=2)
-            acc_view = acc[:].rearrange("s (p u t) -> s u p t", u=2, t=2)
-            for u0, u1 in ((0, 1), (1, 2)) if (j == 0 and e > 0) or e == E - 1 else ((0, 2),):
+            h_view = h_pairs[2 * e + j][:].rearrange("s (u p d) -> s u p d", u=2, d=2)
+            acc_view = acc[:].rearrange("s (p u d) -> s u p d", u=2, d=2)
+            opens_a_run = (j == 0 and e > 0) or e == LAST
+            for u0, u1 in ((0, 1), (1, 2)) if opens_a_run else ((0, 2),):
                 nc.scalar.activation(h_view[:, u0:u1], acc_view[:, u0:u1], GELU)
 
+        def turned_view(t0, t1, bank):
+            return bank[:, : 2 * P * (t1 - t0)].rearrange("p (t u s) -> p t u s", u=2, s=P)
+
         def turn(t0, t1, bank):
-            xt = bank[:, : 2 * P * (t1 - t0)].rearrange("p (j u s) -> p j u s", u=2, s=P)
             newest = t1 - 1
             order = [(newest, 0)] + [(t, u) for t in range(t0, newest) for u in range(2)] + [(newest, 1)]
             for t, u in order:
-                pairs = hb[t // 2, t % 2][:].bitcast(F32)
-                nc.tensor.transpose(xt[:, t - t0, u, :], pairs[:, u * P : (u + 1) * P], ident[:])
+                pairs = h_pairs[t][:].bitcast(F32)
+                nc.tensor.transpose(turned_view(t0, t1, bank)[:, t - t0, u, :], pairs[:, u * P : (u + 1) * P], ident[:])
 
         def quantise(t0, t1, bank, copy_out):
-            xt = bank[:, : 2 * P * (t1 - t0)].rearrange("p (j u s) -> p j u s", u=2, s=P)
-            cols = slice(t0 * P, t1 * P)
-            words = ht[:, 4 * cols.start : 4 * cols.stop]
+            slots = slice(t0 * P, t1 * P)
+            values = h_turned[:, 4 * slots.start : 4 * slots.stop]
             copy_out(
-                words.bitcast(F32).rearrange("p (j s u) -> p j s u", s=P, u=2),
-                xt.rearrange("p j u s -> p j s u"),
+                values.bitcast(F32).rearrange("p (t s u) -> p t s u", s=P, u=2),
+                turned_view(t0, t1, bank).rearrange("p t u s -> p t s u"),
             )
-            nc.vector.quantize_mx(out=codes[:, cols].bitcast(FP8X4), scales=scales[:, cols], in_=words)
+            nc.vector.quantize_mx(out=h_codes[:, slots].bitcast(FP8X4), scales=h_scales[:, slots], in_=values)
 
-        def turn_run(pieces):
+        def turn_and_quantise(pieces):
             for t0, t1, bank, copy_out in pieces:
                 turn(t0, t1, bank)
             for t0, t1, bank, copy_out in pieces:
                 quantise(t0, t1, bank, copy_out)
 
-        def layer2_half(e, half, y, cols):
-            slots = slice(e * C + cols.start, e * C + cols.stop)
+        def layer2_half(e, half, y, ranks):
+            slots = slice(e * C + ranks.start * U, e * C + ranks.stop * U)
             nc.tensor.matmul_mx(
                 out=y,
                 lhsT=w2w[:, e, 2 * P * half : 2 * P * (half + 1)].bitcast(FP4X4),
                 lhsT_scale=w2s[:, e, P * half : P * (half + 1)],
-                rhs=codes[:, slots].bitcast(FP8X4),
-                rhs_scale=scales[:, slots],
+                rhs=h_codes[:, slots].bitcast(FP8X4),
+                rhs_scale=h_scales[:, slots],
                 start=True,
                 stop=True,
             )
@@ -178,12 +192,12 @@ def tile_moe_pke_mlp_gelu_kernel(
         def out_rows(half):
             return out[P * half : P * (half + 1), :].rearrange("p (m c) -> p m c", m=R)
 
-        def layer2(e, bank, copy_out):
+        def layer2(e, bank):
             g = group_of(STORE_GROUPS, e)
             e0, e1 = STORE_GROUPS[g]
             for half in range(2):
-                layer2_half(e, half, bank[:, half * C : (half + 1) * C], slice(0, C))
-            copy_out(
+                layer2_half(e, half, bank[:, half * C : (half + 1) * C], slice(0, R))
+            nc.scalar.copy(
                 stage[g][:, :, :, (e - e0) * U : (e - e0 + 1) * U],
                 bank[:].rearrange("p (h m u) -> p h m u", h=2, u=U),
             )
@@ -191,71 +205,77 @@ def tile_moe_pke_mlp_gelu_kernel(
                 for half in range(2):
                     nc.sync.dma_start(out_rows(half)[:, :, e0 * U : e1 * U], stage[g][:, half, :, :])
 
-        def layer2_last(j, two_banks, copies, queues):
-            e = E - 1
-            for half in range(2):
-                y = two_banks[half][:, half * P : (half + 1) * P]
-                layer2_half(e, half, y, slice(j * P, (j + 1) * P))
-                ranks = slice(2 * j, 2 * j + 2)
-                copies[half](stage[-1][:, half, ranks, U:], y.rearrange("p (m u) -> p m u", u=U))
-                queues[half].dma_start(out_rows(half)[:, ranks, (e - 1) * U : E * U], stage[-1][:, half, ranks, :])
-
-        def flat(tile):
-            return tile[:].rearrange("p g i -> p (g i)")
+        def layer2_split(e, ranks, two_banks, queues):
+            e0, e1 = STORE_GROUPS[-1]
+            for half, copy_out in enumerate((nc.vector.tensor_copy, nc.scalar.copy)):
+                y = two_banks[half][:, : (ranks.stop - ranks.start) * U]
+                layer2_half(e, half, y, ranks)
+                staged = stage[-1][:, half, ranks, :]
+                copy_out(staged[:, :, (e - e0) * U : (e - e0 + 1) * U], y.rearrange("p (m u) -> p m u", u=U))
+                if e == e1 - 1:
+                    queues[half].dma_start(out_rows(half)[:, ranks, e0 * U : e1 * U], staged)
 
         nc.sync.dma_start(lists[:], offs)
-        zero(xs[:, :T])
-        load_xs_pass0(0, nc.sync)
-        load_xs_pass0(1, nc.sync)
-        load_xs_rest(0, nc.scalar)
-        load_xs_rest(1, nc.scalar)
-        load_xs_pass0(2, nc.sync)
-        load_xs_pass0(3, nc.scalar)
-        nc.sync.dma_start(xw01[:], x_words[0:2].rearrange("a p t r -> p a (t r)").bitcast(I32))
+        zero(x_scale_window[:, :T])
+        load_x_scales_pass0(0, nc.sync)
+        load_x_scales_pass0(1, nc.sync)
+        load_x_scales_passes12(0, nc.scalar)
+        load_x_scales_passes12(1, nc.scalar)
+        load_x_scales_pass0(2, nc.sync)
+        load_x_scales_pass0(3, nc.scalar)
+        nc.sync.dma_start(x_words01[:], x_words[0:2].rearrange("a p t r -> p a (t r)").bitcast(I32))
         nc.vector.memset(ident[:], 0.0)
         make_identity(nc, ident[:], nomemset=True)
-        zero(flat(w1s[0]))
-        zero(xs[:, T:])
-        zero(flat(w1s[1]))
+        zero(flat(w1s_tiles[0]))
+        zero(x_scale_window[:, T:])
+        zero(flat(w1s_tiles[1]))
+        zero(flat(w1s_tiles[2]))
         zero(flat(w2s))
         load_w1_words(0)
         load_w1_scales(0)
-        nc.sync.dma_start(xw2[:], x_words[2].rearrange("p t r -> p (t r)").bitcast(I32))
-        gather_scales(0)
+        nc.sync.dma_start(x_words2[:], x_words[2].rearrange("p t r -> p (t r)").bitcast(I32))
         load_w1_words(1)
+        gather_scales(0)
         load_w1_scales(1)
         load_w1_words(2)
+        load_w1_scales(2)
         load_w1_words(3)
         gather_words(0)
         gather_words(1)
 
-        on_scalar, on_vector = nc.scalar.copy, nc.vector.tensor_copy
         for e in range(E):
             layer1(e, 0)
+            if e == LAST:
+                layer2(e - LAG, acc_bank(e - 1, 1))
             if e == 2:
                 gather_scales(1)
-                load_w1_words(5)
-                load_w1_words(6)
             layer1(e, 1)
             if e == 0:
-                load_w2_scales(nc.sync)
-                nc.sync.dma_start(w2w[:].bitcast(I32), w2_words.rearrange("e s p b -> p (e s) b").bitcast(I32))
-            if e == 1:
-                load_w1_scales(2)
+                load_w2()
                 load_w1_words(4)
+            if e == 2:
+                load_w1_scales(3)
+                load_w1_words(5)
+                load_w1_scales(4)
+                load_w1_words(6)
             if e == 3:
                 gather_scales(2)
-                load_w1_scales(3)
-            if e + 2 < E:
+            if e + 2 < LAST:
                 gather_words(e + 2)
+            if e + 2 == LAST:
+                gather_words(LAST, 0, P)
+            if e + 1 == LAST:
+                gather_words(LAST, P, C)
             if e == 1:
-                turn_run([(1, 3, banks[5], on_scalar), (0, 1, acc_bank(1, 0), on_scalar)])
+                turn_and_quantise([(1, 3, banks[5], nc.scalar.copy), (0, 1, acc_bank(1, 0), nc.scalar.copy)])
             if e >= 2:
-                turn_run([(2 * e - 1, 2 * e + 1, banks[4 + e % 2], on_vector if e == E - 1 else on_scalar)])
-            if e >= 3:
-                layer2(e - 3, acc_bank(e, 0), on_scalar)
-        layer2(5, banks[1], on_vector)
-        turn_run([(15, 16, banks[6], on_scalar)])
-        layer2(6, banks[7], on_scalar)
-        layer2_last(0, (banks[0], banks[0]), (on_vector, on_vector), (nc.sync, nc.sync))
-        layer2_last(1, (banks[3], banks[4]), (on_vector, on_scalar), (nc.sync, nc.scalar))
+                copy_out = nc.vector.tensor_copy if e == LAST else nc.scalar.copy
+                turn_and_quantise([(2 * e - 1, 2 * e + 1, banks[4 + e % 2], copy_out)])
+            if LAG <= e < LAST:
+                layer2(e - LAG, acc_bank(e, 0))
+
+        layer2(LAST - 2, acc_bank(LAST, 0))
+        turn_and_quantise([(2 * E - 1, 2 * E, banks[6], nc.scalar.copy)])
+        layer2_split(LAST - 1, slice(0, R), (banks[7], banks[1]), ())
+        layer2_split(LAST, slice(0, 2), (banks[0], banks[2]), (nc.sync, nc.sync))
+        layer2_split(LAST, slice(2, R), (banks[3], banks[4]), (nc.sync, nc.scalar))

@@ -39,7 +39,7 @@ def tile_moe_pke_mlp_gelu_kernel(
         psum = ctx.enter_context(tc.psum_pool(name="psum", bufs=1))
 
         def sbuf(shape, dtype, name):
-            return keep.tile(shape, dtype, name=name, align_bytes=64)
+            return keep.tile(shape, dtype, name=name, align_bytes=256)
 
         banks = [psum.tile([P, 512], F32, name=f"bank{b}") for b in range(8)]
         lists = keep.tile([P, S // 16], U16, name="lists")

@@ -148,7 +148,7 @@ def tile_moe_pke_mlp_gelu_kernel(
                 )
             h_view = h_pairs[2 * e + j][:].rearrange("s (u p d) -> s u p d", u=2, d=2)
             acc_view = acc[:].rearrange("s (p u d) -> s u p d", u=2, d=2)
-            opens_a_run = (j == 0 and e > 0) or e == LAST
+            opens_a_run = (j == 0 and e in (1, 3, 5, 6)) or e == LAST
             for u0, u1 in ((0, 1), (1, 2)) if opens_a_run else ((0, 2),):
                 nc.scalar.activation(h_view[:, u0:u1], acc_view[:, u0:u1], GELU)
 
@@ -268,11 +268,18 @@ def tile_moe_pke_mlp_gelu_kernel(
                 gather_words(LAST, P, C)
             if e == 1:
                 turn_and_quantise([(1, 3, banks[5], nc.scalar.copy), (0, 1, acc_bank(1, 0), nc.scalar.copy)])
-            if e >= 2:
+            if e == 5:
+                layer2(1, acc_bank(e, 0))
+            if e in (3, 5):
+                second_copy = nc.scalar.copy if e == 3 else nc.vector.tensor_copy
+                turn_and_quantise(
+                    [(2 * e - 1, 2 * e + 1, banks[4], nc.scalar.copy), (2 * e - 3, 2 * e - 1, banks[5], second_copy)]
+                )
+            if e >= 6:
                 copy_out = nc.vector.tensor_copy if e == LAST else nc.scalar.copy
                 turn_and_quantise([(2 * e - 1, 2 * e + 1, banks[4 + e % 2], copy_out)])
-            if LAG <= e < LAST:
-                layer2(e - LAG, acc_bank(e, 0))
+            if e in (3, 5, 6):
+                layer2(e - LAG, acc_bank(e, 1 if e == 5 else 0))
 
         layer2(LAST - 2, acc_bank(LAST, 0))
         turn_and_quantise([(2 * E - 1, 2 * E, banks[6], nc.scalar.copy)])

@@ -21,6 +21,7 @@ PASSES = K // 512
 S = E * C
 U = C // R
 LAST = E - 1
+WORD_SET = (0, 1, 2, 0, 1, 2, 1, 2)
 LAG = 3
 
 SCALE_GATHERS = ((0, 4), (4, 6), (6, 8))
@@ -44,17 +45,15 @@ def tile_moe_pke_mlp_gelu_kernel(
         banks = [psum.tile([P, 512], F32, name=f"bank{b}") for b in range(8)]
         lists = keep.tile([P, S // 16], U16, name="lists")
         x_scale_window = sbuf([P, WINDOW], U8, "x_scale_window")
-        x_words01 = sbuf([P, 2, T], I32, "x_words01")
-        x_words2 = sbuf([P, T], I32, "x_words2")
-        word_windows = [x_words01[:, 0, :], x_words01[:, 1, :], x_words2[:]]
+        x_word_rows = sbuf([P, PASSES, T], I32, "x_word_rows")
         w1w = [sbuf([P, (e1 - e0) * PASSES, 2 * H], U8, f"w1w{e0}") for e0, e1 in W1_WORD_GROUPS]
         w1s_tiles = [sbuf([P, (e1 - e0) * PASSES, H], U8, f"w1s{e0}") for e0, e1 in W1_SCALE_GROUPS[:3]]
         w1s = w1s_tiles + [w1s_tiles[1], w1s_tiles[0]]
         w2w = sbuf([P, E, 2 * N], U8, "w2w")
         w2s = sbuf([P, E, N], U8, "w2s")
-        picked_words = [[sbuf([P, C], U32, f"picked_words{s}_{i}") for i in range(PASSES)] for s in range(2)]
-        picked_scales = sbuf([P, 6 * C - P], U8, "picked_scales")
-        picked_scales_start = (0, P, 4 * C - P)
+        picked_words = [[sbuf([P, C], U32, f"picked_words{s}_{i}") for i in range(PASSES)] for s in range(3)]
+        picked_scales = sbuf([P, 5 * C], U8, "picked_scales")
+        picked_scales_start = (C, P, 2 * C + P)
         moved_planes = [sbuf([P, S], U8, f"moved_plane{a}") for a in (1, 2)]
         ident = sbuf([P, P], F32, "ident")
         h_pairs = [sbuf([P, H], BF16, f"h_pairs{t}") for t in range(2 * E)]
@@ -102,13 +101,11 @@ def tile_moe_pke_mlp_gelu_kernel(
         def pass_order(e):
             return (0, 1, 2) if e == 0 else (2, 1, 0)
 
-        def word_buffers(e, j):
-            return picked_words[0] if (e, j) == (LAST, 1) else picked_words[e % 2]
-
-        def gather_words(e, c0=0, c1=C):
+        def gather_words(e):
             for i, a in enumerate(pass_order(e)):
-                picked = word_windows[a].bitcast(U32).indirect(offsets(e * C + c0, e * C + c1))
-                nc.vector.tensor_copy(word_buffers(e, c0 // P)[i][:, c0:c1], picked)
+                end = max((a + 1) * T, 2 * T + 8) if e == 2 else (a + 1) * T
+                picked = flat(x_word_rows)[:, a * T : end].bitcast(U32).indirect(offsets(e * C, (e + 1) * C))
+                nc.vector.tensor_copy(picked_words[WORD_SET[e]][i][:], picked)
 
         def gather_scales(g):
             e0, e1 = SCALE_GATHERS[g]
@@ -139,7 +136,7 @@ def tile_moe_pke_mlp_gelu_kernel(
             for i, a in enumerate(pass_order(e)):
                 nc.tensor.matmul_mx(
                     out=acc[:],
-                    lhsT=word_buffers(e, j)[i][:, j * P : (j + 1) * P].bitcast(FP8X4),
+                    lhsT=picked_words[WORD_SET[e]][i][:, j * P : (j + 1) * P].bitcast(FP8X4),
                     lhsT_scale=x_plane(a, e, j),
                     rhs=w1w[gw][:, (e - W1_WORD_GROUPS[gw][0]) * PASSES + a, :].bitcast(FP4X4),
                     rhs_scale=w1s[gs][:, (e - W1_SCALE_GROUPS[gs][0]) * PASSES + a, :],
@@ -148,7 +145,7 @@ def tile_moe_pke_mlp_gelu_kernel(
                 )
             h_view = h_pairs[2 * e + j][:].rearrange("s (u p d) -> s u p d", u=2, d=2)
             acc_view = acc[:].rearrange("s (p u d) -> s u p d", u=2, d=2)
-            opens_a_run = (j == 0 and e in (1, 3, 5, 6)) or e == LAST
+            opens_a_run = (j == 0 and e not in (0, 4)) or e == LAST
             for u0, u1 in ((0, 1), (1, 2)) if opens_a_run else ((0, 2),):
                 nc.scalar.activation(h_view[:, u0:u1], acc_view[:, u0:u1], GELU)
 
@@ -192,12 +189,12 @@ def tile_moe_pke_mlp_gelu_kernel(
         def out_rows(half):
             return out[P * half : P * (half + 1), :].rearrange("p (m c) -> p m c", m=R)
 
-        def layer2(e, bank):
+        def layer2(e, bank, copy_out=nc.scalar.copy):
             g = group_of(STORE_GROUPS, e)
             e0, e1 = STORE_GROUPS[g]
             for half in range(2):
                 layer2_half(e, half, bank[:, half * C : (half + 1) * C], slice(0, R))
-            nc.scalar.copy(
+            copy_out(
                 stage[g][:, :, :, (e - e0) * U : (e - e0 + 1) * U],
                 bank[:].rearrange("p (h m u) -> p h m u", h=2, u=U),
             )
@@ -223,7 +220,7 @@ def tile_moe_pke_mlp_gelu_kernel(
         load_x_scales_passes12(1, nc.scalar)
         load_x_scales_pass0(2, nc.sync)
         load_x_scales_pass0(3, nc.scalar)
-        nc.sync.dma_start(x_words01[:], x_words[0:2].rearrange("a p t r -> p a (t r)").bitcast(I32))
+        nc.sync.dma_start(x_word_rows[:, 0:2, :], x_words[0:2].rearrange("a p t r -> p a (t r)").bitcast(I32))
         nc.vector.memset(ident[:], 0.0)
         make_identity(nc, ident[:], nomemset=True)
         zero(flat(w1s_tiles[0]))
@@ -233,7 +230,7 @@ def tile_moe_pke_mlp_gelu_kernel(
         zero(flat(w2s))
         load_w1_words(0)
         load_w1_scales(0)
-        nc.sync.dma_start(x_words2[:], x_words[2].rearrange("p t r -> p (t r)").bitcast(I32))
+        nc.sync.dma_start(x_word_rows[:, 2, :], x_words[2].rearrange("p t r -> p (t r)").bitcast(I32))
         load_w1_words(1)
         gather_scales(0)
         load_w1_scales(1)
@@ -242,13 +239,14 @@ def tile_moe_pke_mlp_gelu_kernel(
         load_w1_words(3)
         gather_words(0)
         gather_words(1)
+        gather_words(2)
 
         for e in range(E):
             layer1(e, 0)
             if e == LAST:
-                layer2(e - LAG, acc_bank(e - 1, 1))
-            if e == 2:
-                gather_scales(1)
+                layer2(e - LAG, acc_bank(e - 1, 1), nc.vector.tensor_copy)
+            if e in (1, 3):
+                gather_scales(1 + e // 2)
             layer1(e, 1)
             if e == 0:
                 load_w2()
@@ -258,28 +256,19 @@ def tile_moe_pke_mlp_gelu_kernel(
                 load_w1_words(5)
                 load_w1_scales(4)
                 load_w1_words(6)
-            if e == 3:
-                gather_scales(2)
-            if e + 2 < LAST:
+            if e < 3:
+                gather_words(e + 3)
+            if e in (4, 5):
                 gather_words(e + 2)
-            if e + 2 == LAST:
-                gather_words(LAST, 0, P)
-            if e + 1 == LAST:
-                gather_words(LAST, P, C)
             if e == 1:
                 turn_and_quantise([(1, 3, banks[5], nc.scalar.copy), (0, 1, acc_bank(1, 0), nc.scalar.copy)])
             if e == 5:
-                layer2(1, acc_bank(e, 0))
-            if e in (3, 5):
-                second_copy = nc.scalar.copy if e == 3 else nc.vector.tensor_copy
-                turn_and_quantise(
-                    [(2 * e - 1, 2 * e + 1, banks[4], nc.scalar.copy), (2 * e - 3, 2 * e - 1, banks[5], second_copy)]
-                )
-            if e >= 6:
+                turn_and_quantise([(9, 11, banks[4], nc.scalar.copy), (7, 9, banks[5], nc.vector.tensor_copy)])
+            if e in (2, 3, 6, 7):
                 copy_out = nc.vector.tensor_copy if e == LAST else nc.scalar.copy
                 turn_and_quantise([(2 * e - 1, 2 * e + 1, banks[4 + e % 2], copy_out)])
-            if e in (3, 5, 6):
-                layer2(e - LAG, acc_bank(e, 1 if e == 5 else 0))
+            if LAG <= e < LAST:
+                layer2(e - LAG, acc_bank(e, 0), nc.scalar.copy if e < LAST - 1 else nc.vector.tensor_copy)
 
         layer2(LAST - 2, acc_bank(LAST, 0))
         turn_and_quantise([(2 * E - 1, 2 * E, banks[6], nc.scalar.copy)])

@@ -265,7 +265,7 @@ def tile_moe_pke_mlp_gelu_kernel(
             if e == 5:
                 turn_and_quantise([(9, 11, banks[4], nc.scalar.copy), (7, 9, banks[5], nc.vector.tensor_copy)])
             if e in (2, 3, 6, 7):
-                copy_out = nc.vector.tensor_copy if e == LAST else nc.scalar.copy
+                copy_out = nc.vector.tensor_copy if e >= LAST - 1 else nc.scalar.copy
                 turn_and_quantise([(2 * e - 1, 2 * e + 1, banks[4 + e % 2], copy_out)])
             if LAG <= e < LAST:
                 layer2(e - LAG, acc_bank(e, 0), nc.scalar.copy if e < LAST - 1 else nc.vector.tensor_copy)

from contextlib import ExitStack

import concourse.mybir as mybir
from concourse.masks import make_identity

K, T, E, C, H, N, R = 1536, 768, 8, 256, 512, 256, 4
FLOPS = 2 * E * C * (K * H + H * N)

F32 = mybir.dt.float32
BF16 = mybir.dt.bfloat16
I32 = mybir.dt.int32
U32 = mybir.dt.uint32
U16 = mybir.dt.uint16
U8 = mybir.dt.uint8
FP8X4 = mybir.dt.float8_e4m3fn_x4
FP4X4 = mybir.dt.float4_e2m1fn_x4
GELU = mybir.ActivationFunctionType.Gelu_apprx_tanh

P = 128
PASSES = K // 512
S = E * C
U = C // R
LAST = E - 1
WORD_SET = (0, 1, 2, 0, 1, 2, 1, 2)
LAG = 3

SCALE_GATHERS = ((0, 4), (4, 6), (6, 8))
WINDOW = 1408
W1_WORD_GROUPS = ((0, 1), (1, 2), (2, 3), (3, 4), (4, 5), (5, 6), (6, 8))
W1_SCALE_GROUPS = ((0, 1), (1, 3), (3, 5), (5, 7), (7, 8))
STORE_GROUPS = ((0, 3), (3, 5), (5, 6), (6, 8))


def tile_moe_pke_mlp_gelu_kernel(
    tc, x_words, x_scales, w1_words, w1_scales, w2_words, w2_scales, offs, out
):
    nc = tc.nc
    with ExitStack() as ctx:
        keep = ctx.enter_context(tc.tile_pool(name="keep", bufs=1))
        psum = ctx.enter_context(tc.psum_pool(name="psum", bufs=1))

        def sbuf(shape, dtype, name):
            return keep.tile(shape, dtype, name=name, align_bytes=256)

        banks = [psum.tile([P, 512], F32, name=f"bank{b}") for b in range(8)]
        lists = keep.tile([P, S // 16], U16, name="lists")
        x_scale_window = sbuf([P, WINDOW], U8, "x_scale_window")
        x_word_rows = sbuf([P, PASSES, T], I32, "x_word_rows")
        w1w = [sbuf([P, (e1 - e0) * PASSES, 2 * H], U8, f"w1w{e0}") for e0, e1 in W1_WORD_GROUPS]
        w1s_tiles = [sbuf([P, (e1 - e0) * PASSES, H], U8, f"w1s{e0}") for e0, e1 in W1_SCALE_GROUPS[:3]]
        w1s = w1s_tiles + [w1s_tiles[1], w1s_tiles[0]]
        w2w = sbuf([P, E, 2 * N], U8, "w2w")
        w2s = sbuf([P, E, N], U8, "w2s")
        picked_words = [[sbuf([P, C], U32, f"picked_words{s}_{i}") for i in range(PASSES)] for s in range(3)]
        picked_scales = sbuf([P, 5 * C], U8, "picked_scales")
        picked_scales_start = (C, P, 2 * C + P)
        moved_planes = [sbuf([P, S], U8, f"moved_plane{a}") for a in (1, 2)]
        ident = sbuf([P, P], F32, "ident")
        h_pairs = [sbuf([P, H], BF16, f"h_pairs{t}") for t in range(2 * E)]
        h_turned = sbuf([P, 4 * S], BF16, "h_turned")
        h_codes = sbuf([P, S], U32, "h_codes")
        h_scales = sbuf([P, S], U8, "h_scales")
        stage = [keep.tile([P, 2, R, (e1 - e0) * U], F32, name=f"stage{e0}") for e0, e1 in STORE_GROUPS]

        def group_of(groups, e):
            return [g for g, (e0, e1) in enumerate(groups) if e0 <= e < e1][0]

        def zero(ap):
            nc.vector.memset(ap.bitcast(I32), 0)

        def flat(tile):
            return tile[:].rearrange("p g i -> p (g i)")

        def load_x_scales_pass0(quadrant, queue):
            rows = x_scales[0, 4 * quadrant : 4 * quadrant + 4, :]
            queue.dma_start(x_scale_window[32 * quadrant : 32 * quadrant + 4, :T].bitcast(I32), rows.bitcast(I32))

        def load_x_scales_passes12(q, queue):
            rows = x_scales.rearrange("a (h q r) t -> (a h) q r t", h=2, q=2)[2:6, q]
            queue.dma_start(x_scale_window[32 * q + 4 : 32 * q + 20, :T].bitcast(I32), rows.bitcast(I32))

        def load_w1_scales(g):
            e0, e1 = W1_SCALE_GROUPS[g]
            rows = w1_scales[e0:e1].rearrange("e s (q r) i -> r q (e s) i", r=4)
            for r in range(4):
                nc.sync.dma_start(w1s[g][r:P:32].bitcast(I32), rows[r].bitcast(I32))

        def load_w2():
            rows = w2_scales.rearrange("e s (q r) n -> r q (e s) n", r=4)
            for r in range(4):
                nc.sync.dma_start(w2s[r:P:32].bitcast(I32), rows[r].bitcast(I32))
            nc.sync.dma_start(w2w[:].bitcast(I32), w2_words.rearrange("e s p b -> p (e s) b").bitcast(I32))

        def load_w1_words(g):
            e0, e1 = W1_WORD_GROUPS[g]
            nc.sync.dma_start(w1w[g][:].bitcast(I32), w1_words[e0:e1].rearrange("e s p b -> p (e s) b").bitcast(I32))

        def offsets(s0, s1):
            return lists[:, s0 // 16 : s1 // 16]

        def pass_order(e):
            return (0, 1, 2) if e == 0 else (2, 1, 0)

        def gather_words(e):
            for i, a in enumerate(pass_order(e)):
                end = max((a + 1) * T, 2 * T + 8) if e == 2 else (a + 1) * T
                picked = flat(x_word_rows)[:, a * T : end].bitcast(U32).indirect(offsets(e * C, (e + 1) * C))
                nc.vector.tensor_copy(picked_words[WORD_SET[e]][i][:], picked)

        def gather_scales(g):
            e0, e1 = SCALE_GATHERS[g]
            s0, s1 = e0 * C, e1 * C
            cols = slice(picked_scales_start[g], picked_scales_start[g] + s1 - s0)
            nc.vector.tensor_copy(picked_scales[:, cols], x_scale_window[:].indirect(offsets(s0, s1)))
            for a in (1, 2):
                for h in range(2):
                    row = 4 + 8 * (a - 1) + 4 * h
                    nc.sync.dma_start(
                        moved_planes[a - 1][64 * h : 64 * h + 64, s0:s1].bitcast(I32),
                        picked_scales[row : row + 64, cols].bitcast(I32),
                    )

        def x_plane(a, e, j):
            if a == 0:
                g = group_of(SCALE_GATHERS, e)
                c0 = picked_scales_start[g] + (e - SCALE_GATHERS[g][0]) * C + j * P
                return picked_scales[:, c0 : c0 + P]
            return moved_planes[a - 1][:, e * C + j * P : e * C + (j + 1) * P]

        def acc_bank(e, j):
            return banks[2 * (e % 2) + j]

        def layer1(e, j):
            gw, gs = group_of(W1_WORD_GROUPS, e), group_of(W1_SCALE_GROUPS, e)
            acc = acc_bank(e, j)
            for i, a in enumerate(pass_order(e)):
                nc.tensor.matmul_mx(
                    out=acc[:],
                    lhsT=picked_words[WORD_SET[e]][i][:, j * P : (j + 1) * P].bitcast(FP8X4),
                    lhsT_scale=x_plane(a, e, j),
                    rhs=w1w[gw][:, (e - W1_WORD_GROUPS[gw][0]) * PASSES + a, :].bitcast(FP4X4),
                    rhs_scale=w1s[gs][:, (e - W1_SCALE_GROUPS[gs][0]) * PASSES + a, :],
                    start=(i == 0),
                    stop=(i == PASSES - 1),
                )
            h_view = h_pairs[2 * e + j][:].rearrange("s (u p d) -> s u p d", u=2, d=2)
            acc_view = acc[:].rearrange("s (p u d) -> s u p d", u=2, d=2)
            opens_a_run = (j == 0 and e not in (0, 4)) or e == LAST
            for u0, u1 in ((0, 1), (1, 2)) if opens_a_run else ((0, 2),):
                nc.scalar.activation(h_view[:, u0:u1], acc_view[:, u0:u1], GELU)

        def turned_view(t0, t1, bank):
            return bank[:, : 2 * P * (t1 - t0)].rearrange("p (t u s) -> p t u s", u=2, s=P)

        def turn(t0, t1, bank):
            newest = t1 - 1
            order = [(newest, 0)] + [(t, u) for t in range(t0, newest) for u in range(2)] + [(newest, 1)]
            for t, u in order:
                pairs = h_pairs[t][:].bitcast(F32)
                nc.tensor.transpose(turned_view(t0, t1, bank)[:, t - t0, u, :], pairs[:, u * P : (u + 1) * P], ident[:])

        def quantise(t0, t1, bank, copy_out):
            slots = slice(t0 * P, t1 * P)
            values = h_turned[:, 4 * slots.start : 4 * slots.stop]
            copy_out(
                values.bitcast(F32).rearrange("p (t s u) -> p t s u", s=P, u=2),
                turned_view(t0, t1, bank).rearrange("p t u s -> p t s u"),
            )
            nc.vector.quantize_mx(out=h_codes[:, slots].bitcast(FP8X4), scales=h_scales[:, slots], in_=values)

        def turn_and_quantise(pieces):
            for t0, t1, bank, copy_out in pieces:
                turn(t0, t1, bank)
            for t0, t1, bank, copy_out in pieces:
                quantise(t0, t1, bank, copy_out)

        def layer2_half(e, half, y, ranks):
            slots = slice(e * C + ranks.start * U, e * C + ranks.stop * U)
            nc.tensor.matmul_mx(
                out=y,
                lhsT=w2w[:, e, 2 * P * half : 2 * P * (half + 1)].bitcast(FP4X4),
                lhsT_scale=w2s[:, e, P * half : P * (half + 1)],
                rhs=h_codes[:, slots].bitcast(FP8X4),
                rhs_scale=h_scales[:, slots],
                start=True,
                stop=True,
            )

        def out_rows(half):
            return out[P * half : P * (half + 1), :].rearrange("p (m c) -> p m c", m=R)

        def layer2(e, bank, copy_out=nc.scalar.copy):
            g = group_of(STORE_GROUPS, e)
            e0, e1 = STORE_GROUPS[g]
            for half in range(2):
                layer2_half(e, half, bank[:, half * C : (half + 1) * C], slice(0, R))
            copy_out(
                stage[g][:, :, :, (e - e0) * U : (e - e0 + 1) * U],
                bank[:].rearrange("p (h m u) -> p h m u", h=2, u=U),
            )
            if e == e1 - 1:
                for half in range(2):
                    nc.sync.dma_start(out_rows(half)[:, :, e0 * U : e1 * U], stage[g][:, half, :, :])

        def layer2_split(e, ranks, two_banks, queues):
            e0, e1 = STORE_GROUPS[-1]
            for half, copy_out in enumerate((nc.vector.tensor_copy, nc.scalar.copy)):
                y = two_banks[half][:, : (ranks.stop - ranks.start) * U]
                layer2_half(e, half, y, ranks)
                staged = stage[-1][:, half, ranks, :]
                copy_out(staged[:, :, (e - e0) * U : (e - e0 + 1) * U], y.rearrange("p (m u) -> p m u", u=U))
                if e == e1 - 1:
                    queues[half].dma_start(out_rows(half)[:, ranks, e0 * U : e1 * U], staged)

        nc.sync.dma_start(lists[:], offs)
        zero(x_scale_window[:, :T])
        load_x_scales_pass0(0, nc.sync)
        load_x_scales_pass0(1, nc.sync)
        load_x_scales_passes12(0, nc.scalar)
        load_x_scales_passes12(1, nc.scalar)
        load_x_scales_pass0(2, nc.sync)
        load_x_scales_pass0(3, nc.scalar)
        nc.sync.dma_start(x_word_rows[:, 0:2, :], x_words[0:2].rearrange("a p t r -> p a (t r)").bitcast(I32))
        nc.vector.memset(ident[:], 0.0)
        make_identity(nc, ident[:], nomemset=True)
        zero(flat(w1s_tiles[0]))
        zero(x_scale_window[:, T:])
        zero(flat(w1s_tiles[1]))
        zero(flat(w1s_tiles[2]))
        zero(flat(w2s))
        load_w1_words(0)
        load_w1_scales(0)
        nc.sync.dma_start(x_word_rows[:, 2, :], x_words[2].rearrange("p t r -> p (t r)").bitcast(I32))
        load_w1_words(1)
        gather_scales(0)
        load_w1_scales(1)
        load_w1_words(2)
        load_w1_scales(2)
        load_w1_words(3)
        gather_words(0)
        gather_words(1)
        gather_words(2)

        for e in range(E):
            layer1(e, 0)
            if e == LAST:
                layer2(e - LAG, acc_bank(e - 1, 1), nc.vector.tensor_copy)
            if e in (1, 3):
                gather_scales(1 + e // 2)
            layer1(e, 1)
            if e == 0:
                load_w2()
                load_w1_words(4)
            if e == 2:
                load_w1_scales(3)
                load_w1_words(5)
                load_w1_scales(4)
                load_w1_words(6)
            if e < 3:
                gather_words(e + 3)
            if e in (4, 5):
                gather_words(e + 2)
            if e == 1:
                turn_and_quantise([(1, 3, banks[5], nc.scalar.copy), (0, 1, acc_bank(1, 0), nc.scalar.copy)])
            if e == 5:
                turn_and_quantise([(9, 11, banks[4], nc.scalar.copy), (7, 9, banks[5], nc.vector.tensor_copy)])
            if e in (2, 3, 6, 7):
                copy_out = nc.vector.tensor_copy if e >= LAST - 1 else nc.scalar.copy
                turn_and_quantise([(2 * e - 1, 2 * e + 1, banks[4 + e % 2], copy_out)])
            if LAG <= e < LAST:
                layer2(e - LAG, acc_bank(e, 0), nc.scalar.copy if e < LAST - 1 else nc.vector.tensor_copy)

        layer2(LAST - 2, acc_bank(LAST, 0))
        turn_and_quantise([(2 * E - 1, 2 * E, banks[6], nc.scalar.copy)])
        layer2_split(LAST - 1, slice(0, R), (banks[7], banks[1]), ())
        layer2_split(LAST, slice(0, 2), (banks[0], banks[2]), (nc.sync, nc.sync))
        layer2_split(LAST, slice(2, R), (banks[3], banks[4]), (nc.sync, nc.scalar))
